import numpy as np, ml_dtypes
CORES = [66,74,82,90,194,202,210,218]
N = 8
import mx_ref
BF = ml_dtypes.bfloat16
def gentries(a):
    return np.ascontiguousarray(a.reshape(8, 16, -1).transpose(0, 2, 1)).reshape(8, -1)
def gtable(e):
    e = np.asarray(e); return np.ascontiguousarray(e.reshape(8, -1, 16).transpose(0, 2, 1)).reshape(128, -1).astype(np.int32)
def gcols(t, e):
    v = np.concatenate([t.reshape(8, 16, -1, 4), np.zeros((8, 16, 1, 4), BF)], axis=2)
    return np.ascontiguousarray(np.stack([v[g][:, e[g]] for g in range(8)])).reshape(128, -1)
def tile(rs):
    return np.stack(rs, axis=2).reshape(128, -1).astype(BF)
def pick(q, e):
    c = np.concatenate([q[0].reshape(128, -1, 4), np.zeros((128, 1, 4), np.uint8)], axis=1); s = np.concatenate([q[1], np.ones((16, 1), np.uint8)], axis=1)
    return (np.ascontiguousarray(c[:, e].reshape(128, -1)), np.ascontiguousarray(s[:, e]))
def join(*qs):
    return (np.concatenate([q[0] for q in qs], axis=1), np.concatenate([q[1] for q in qs], axis=1))
def put(q, e, v):
    c, s = q[0].reshape(128, -1, 4).copy(), q[1].copy(); c[:, e] = v[0].reshape(128, -1, 4); s[:, e] = v[1]
    return (c.reshape(128, -1), s)
def pk(c, s):
    return (np.ascontiguousarray(c), mx_ref.live(s))
def emit(q):
    return q[0], q[1]
def packed(v, rng):
    q = [mx_ref.quantize(np.ascontiguousarray(v[r])) for r in range(N)]
    return np.stack([a for a, b in q]), np.stack([mx_ref.plane(b, rng) for a, b in q])
def values_of_codes():
    e, c = np.zeros((128, 128, 4), np.float32), np.zeros((128, 2, 4), np.uint8)
    e[np.arange(128), np.arange(128), 0] = 1
    c[:127, :, 0] = np.arange(256).reshape(2, 128).T[:127]
    return mx_ref.matmul(mx_ref.quantize(e.reshape(128, 512).astype(BF)), (c.reshape(128, 8), np.full((16, 2), 127, np.uint8))).T.reshape(-1).astype(np.float64)
CODE_VALUE, SCALE_VALUE = values_of_codes(), 2.0 ** (np.arange(256) - 127.0)
def decode(q):
    return (CODE_VALUE[q[0]].reshape(16, 8, -1, 4) * SCALE_VALUE[q[1]][:, None, :, None] + 0.0).reshape(128, -1).astype(np.float32)
def f(rng, *shape):
    return mx_ref.flush((rng.standard_normal(shape, dtype=np.float32) * np.exp2(rng.integers(-2, 3, shape[:-1] + (1,)))).astype(BF))
def wide(rng, *shape, cols=0):
    v = rng.standard_normal(shape, dtype=np.float32) * np.exp2(rng.integers(-12, 13, shape)).astype(np.float32)
    if cols: v *= np.repeat(np.exp2(rng.integers(-cols, cols + 1, shape[:-2] + (1, shape[-1] // 4))) * (rng.random(shape[:-2] + (1, shape[-1] // 4)) > 0.0625), 4, axis=-1).astype(np.float32)
    return mx_ref.flush(v.astype(BF))
C, HALF = 288, 144
MASK = [4, 1, 2]
def numbers_of(rng):
    return {"x": np.array(f(rng, N, 128, 4 * C)), "u": np.array(f(rng, N, 128, 512)), "v": np.array(f(rng, N, 128, 512))}
def orders(rng):
    e = np.tile(np.arange(C), (N, 8, 1))
    k = [rng.permuted(e, axis=2) for i in range(4)]
    t = np.zeros((N, 8, C), np.int64)
    np.put_along_axis(t, k[3], np.ascontiguousarray(k[3].reshape(N, 8, HALF, 2)[:, :, :, ::-1]).reshape(N, 8, C), axis=2)
    return k[:3] + [t]
def stored(k):
    return {n: np.stack([gtable(a[r]) for r in range(N)]) for n, a in zip(("lg", "pb", "fd", "ex"), k)}
def lists(rng):
    return stored(orders(rng))
def layers(rng):
    return np.array(f(rng, N, 128, 2048)).reshape(N, 8, 16, 4, 8, 16, 4)
def weights(rng, w):
    c, p = packed(np.ascontiguousarray(w).reshape(N, 128, 2048), rng)
    return {"wc": c, "ws": p}
def setup_inputs(rng):
    return {**numbers_of(rng), **lists(rng), **weights(rng, layers(rng))}
def setup_inputs_ties(rng):
    d = numbers_of(rng)
    o = rng.permutation(N)
    k = rng.integers(-1, 2, (N, 8, 4, C)).astype(np.float32)
    k[o[1]] = 1
    k[o[2]] = -1
    x = d["x"].reshape(N, 8, 16, C, 4)
    x[:, :, :4] = 0
    x[:, :, :4, :, 0] = k.astype(BF)
    u = d["u"].reshape(N, 8, 16, 8, 16, 4)
    u[:, :, :, :, :4] = 0
    for g in range(8):
        for j in range(4): u[:, g, j, g, j, 0] = 1.0
    u[o[0], :, :, :, :4] = 0
    w = layers(rng)
    w[:, :, :, :, :, :4] = 0
    return {"x": x.reshape(N, 128, 4 * C), "u": u.reshape(N, 128, 512), "v": d["v"], **lists(rng), **weights(rng, w)}
def setup_inputs_near(rng):
    d = numbers_of(rng)
    o = rng.permutation(N)
    k = np.ones(N, np.float32)
    k[o[:N // 2]] = 2.0 ** -30
    s = rng.integers(-1, 2, (N, 8, 4, C)) * np.where(k < 1, 2 * k, k)[:, None, None, None]
    x = d["x"].astype(np.float32).reshape(N, 8, 16, C, 4)
    x[:, :, :8] = 0
    x[:, :, 0:8:2, :, 0] = 1.125 * s
    x[:, :, 1:8:2, :, 0] = -1.25 * s
    for r in range(N):
        at_ = [0, C - 1, int(rng.integers(C)), int(rng.integers(C))]
        for g, c in zip(rng.permutation(8)[:4], at_): x[r, g, 2 * rng.integers(4), c, 0] = 2.0 ** 30 * rng.choice([-1.0, 1.0])
    x[o[0], :, 8:] = 0
    x[o[0], :, 12:, :, 0] = rng.choice([-1.0, 1.0], (8, 4, C)) * 2.0 ** -30
    x[o[0], :, 12, :, 2] = 2.0 ** -30
    u = d["u"].reshape(N, 8, 16, 8, 16, 4)
    u[:, :, :, :, :4] = 0
    w = np.zeros((N, 8, 16, 4, 8, 16, 4), np.float32)
    for g in range(8):
        for j in range(4):
            u[:, g, 2 * j, g, j, 0] = (1.125 * k).astype(np.float32).astype(BF)
            u[:, g, 2 * j + 1, g, j, 0] = k.astype(BF)
            w[:, g, 12 + j, 0, g, 8 + j, 0] = 1.125 * 2.0 ** -8
            w[:, g, 12 + j, 1, g, 8 + (j + 1) % 4, 0] = -1.25 * 2.0 ** -8
        w[:, g, 12, 1, g, 12, 2] = 2.0 ** 5
    u[o[0], :, :, :, :4] = 0
    for g in range(8):
        for j in range(4):
            u[o[0], g, 8 + j, g, j, 0] = 1.125 * 2.0 ** -30
            u[o[0], g, 8 + (j + 1) % 4, g, j, 1] = 2.0 ** -30
    return {"x": x.reshape(N, 128, 4 * C).astype(BF), "u": u.reshape(N, 128, 512), "v": d["v"], **lists(rng), **weights(rng, w.astype(BF))}
def setup_inputs_odd(rng):
    d = numbers_of(rng)
    x = np.zeros((N, 8, 16, C, 4), np.float32)
    x[:, :, 0, :, 1] = 1.96875 * 2.0 ** 8 * rng.choice([-1.0, 1.0], (N, 8, C))
    x[:, :, :4, :, 0] = -(8 + rng.integers(0, 2, (N, 8, 4, C))) * 2.0 ** -8
    x[:, :, 4:8, :, 0] = 8 * 2.0 ** -8
    a = np.exp2(rng.integers(-3, 4, 8).astype(np.float32))[None, :, None]
    x[:, :, 8, :, 0] = -2.953125 * a
    x[:, :, 12, :, 0] = -1.125 * a
    x[:, :, 14, :, 0] = -0.0703125 * a
    u = d["u"].reshape(N, 8, 16, 8, 16, 4)
    u[:, :, :, :, :4] = 0
    w = np.zeros((N, 8, 16, 4, 8, 16, 4), np.float32)
    for g in range(8):
        for j in range(4):
            u[:, g, j, g, j, 0] = 1.0
            u[:, g, 4 + j, g, j, 0] = 1.0
            w[:, g, 14, j, g, 9, 0] = -2.0 ** (j - 5)
        w[:, g, 12, 0, g, 8, 0] = -28.0
    return {"x": x.reshape(N, 128, 4 * C).astype(BF), "u": u.reshape(N, 128, 512), "v": d["v"], **lists(rng), **weights(rng, w.astype(BF))}
def setup_inputs_ends(rng):
    d = numbers_of(rng)
    o, e = rng.permutation(N) % 4, rng.permutation(N) % 4
    s = rng.choice([-1.0, 1.0], (N, 128, C, 4))
    s[o == 0] = -1
    s[o == 1] = rng.choice([-1.0, 1.0], (N, 1, C, 1))[o == 1]
    for r in range(N):
        if o[r] == 3: s[r, ::8, :, 0] = 1
    x = s * (0.955 + 0.02 * rng.random((N, 128, C, 4))) * 2.0 ** 30
    x[o == 3] = s[o == 3] * 2.0 ** -30
    size = np.where(o == 3, 2.0 ** -30, 2.0 ** 30)
    a = np.stack([rng.permutation(32).reshape(8, 4) % 2 * 2.0 - 1.0 for r in range(N)]) * size[:, None, None]
    u = d["u"].reshape(N, 128, 8, 16, 4)
    u[:, :, :, :4] = a.astype(np.float32).astype(BF)[:, None, :, :, None]
    v = rng.choice([-1.0, 1.0], (N, 128, 512)) * size[:, None, None]
    c = np.arange(C)
    plain, pairs = [c, c[::-1], (c + 1) % C], [c[::-1], c ^ 1, (c + HALF) % C]
    k = orders(rng)
    for r in range(N):
        if e[r] < 3:
            for n in range(3): k[n][r] = plain[(e[r] + n) % 3]
            k[3][r] = pairs[e[r]]
    h = np.where(o == 3, 32.0, -0.125)[:, None] * np.ones((1, 128))
    for r in range(N):
        if o[r] == 3:
            h[r, 14::16] = 2.0 ** -8
            h[r, 15::16] = 2.0 ** 8
        else: h[r, 15::16] = 0
    w = np.zeros((N, 128, 4, 128, 4), np.float32)
    i = np.arange(128)
    for b in range(4): w[:, i, b, i, b] = h
    return {"x": x.astype(np.float32).reshape(N, 128, 4 * C).astype(BF), "u": u.reshape(N, 128, 512), "v": v.astype(np.float32).astype(BF), **stored(k), **weights(rng, w.astype(BF))}
def setup_inputs_spread(rng):
    d = setup_inputs(rng)
    d["x"] = wide(rng, N, 128, 4 * C, cols=6)
    return d
def check_inputs(d):
    b = []
    for k in ("x", "u", "v"):
        a = np.abs(d[k].astype(np.float32))
        if not (np.isfinite(a).all() and ((a == 0) | (a >= 2.0 ** -30) & (a <= 2.0 ** 30)).all()): b.append("a value of " + k)
    for k in ("lg", "pb", "fd"):
        if not (np.sort(d[k].reshape(N, 8, C), axis=2) == np.arange(C)).all(): b.append(k + ": no permutation")
    for r in range(N):
        e = gentries(d["ex"][r])
        if not ((e >= 0) & (e < C)).all(): b.append("an entry of ex")
        elif (e == np.arange(C)).any() or (at(e, e) != np.arange(C)).any(): b.append("ex: no pairs")
    none, least, most = [emit(mx_ref.quantize(np.full((128, 16), k, np.float32).astype(BF)))[1][0, 0] for k in (0.0, 2.0 ** -8, 2.0 ** 8)]
    for r in range(N):
        if ((d["wc"][r] == 0x7F) | (d["wc"][r] == 0xFF)).any(): b.append("wc: a code that is no number")
        s = mx_ref.live(d["ws"][r])
        if ((s != none) & ((s < least) | (s > most))).any(): b.append("ws: a scale out of range")
        if (((d["wc"][r].reshape(16, 8, 512, 4) & 0x7F) != 0) & (s == none)[:, None, :, None]).any(): b.append("wc: a code other than zero under the scale of zeros")
    return b
def at(t, e):
    return np.take_along_axis(t, e.astype(np.int64), axis=1)
def reference(x, u, v, lg, pb, fd, ex, wc, ws):
    qu = [mx_ref.quantize(u[r]) for r in range(N)]
    lay = [pk(wc[r], ws[r]) for r in range(N)]
    leg, back, fore, pair = [[gentries(t[r]) for r in range(N)] for t in (lg, pb, fd, ex)]
    now = [x[r] for r in range(N)]
    for mask in MASK:
        made, swapped = [], []
        for r in range(N):
            s = mx_ref.matmul(qu[r], mx_ref.quantize(now[r])).reshape(8, 16, C)
            low = np.minimum(np.arange(C), pair[r])
            turn = [np.where(at(s[:, j], low) < 0, pair[r], np.arange(C)) for j in range(4)]
            for j, b in enumerate((back[r ^ mask], back[r], back[r ^ mask])):
                leg[r] = at(b, at(turn[j], at(leg[r], fore[r])))
            swapped.append(at(back[r], turn[3]))
            z = (gcols(now[r], leg[r]).astype(np.float32) + gcols(now[r], at(leg[r], fore[r])).astype(np.float32)) * np.float32(0.5)
            q = mx_ref.quantize(z.astype(BF))
            made.append(tile([mx_ref.matmul(pick(lay[r], np.arange(128 * b, 128 * b + 128)), q) * np.float32(0.03125) for b in range(4)]))
        new = []
        for r in range(N):
            m = at(fore[r], leg[r])
            far = gcols(decode(mx_ref.quantize(made[r ^ mask])).astype(BF), m[:, :HALF])
            near = gcols(made[r], m[:, HALF:])
            new.append((now[r].astype(np.float32) + np.concatenate([far, near], axis=1).astype(np.float32)).astype(BF))
        now, back = new, swapped
    y, pl = np.zeros((N, 128, C), np.float32), np.zeros((N, 8, 2 * C), np.float32)
    oc, osc = np.zeros((N, 128, 4 * C), np.uint8), np.zeros((N, 16, C), np.uint8)
    for r in range(N):
        q = mx_ref.quantize(now[r])
        y[r] = mx_ref.matmul(mx_ref.quantize(v[r]), q)
        pl[r] = np.concatenate([leg[r], back[r]], axis=1)
        oc[r], osc[r] = emit(q)
    return {"y": y, "pl": pl, "oc": oc, "osc": osc}

@@ -1,0 +1,500 @@
+from concourse.mybir import dt, AluOpType as Op, ActivationFunctionType as Act
+
+C, HALF = 288, 144
+MASK = [4, 1, 2]
+K = 65536.0
+SLOT = {2: 0, 1: 1, 0: 2, 3: 3}
+_F = {}
+_n = 0
+for _name, _w in (("TM", 288), ("A1", 288), ("A2", 288), ("A0", 288), ("IOT", 288), ("ER", 288), ("FR", 288), ("FF", 288),
+                  ("F3", 288), ("F3S", 288), ("KW", 24), ("CW", 24), ("EXF", 24), ("LOWF", 24), ("D1", 24),
+                  ("PMF", 8), ("PM1", 8), ("T15", 8), ("INV", 8)):
+    _F[_name] = _n
+    _n += _w
+_L = {"pb": 0, "ex": 24, "fd": 48, "lg": 72, "PI": 96, "PM": 104, "UL": 112}
+_U = {"FU": 0, "F3U": 32, "EXU": 64, "LGU": 96, "FH": 160, "ULU": 192}
+
+SCRATCH = {
+    "CF": ("sbuf", [128, _n], "float32"), "LI": ("sbuf", [128, 144], "int32"), "CU": ("sbuf", [128, 224], "uint16"),
+    "ut": ("sbuf", [128, 512], "bfloat16"), "vt": ("sbuf", [128, 512], "bfloat16"),
+    "uq": ("sbuf", [128, 128], "float8_e4m3fn_x4"), "us": ("sbuf", [128, 128], "uint8"),
+    "uq2": ("sbuf", [128, 512], "float8_e4m3fn_x4"), "us2": ("sbuf", [128, 512], "uint8"),
+    "vq": ("sbuf", [128, 128], "float8_e4m3fn_x4"), "vs": ("sbuf", [128, 128], "uint8"),
+    "wq": ("sbuf", [128, 512], "float8_e4m3fn_x4"), "wp": ("sbuf", [128, 512], "uint8"),
+    "ONE": ("sbuf", [128, 512], "bfloat16"), "ET": ("sbuf", [128, 2048], "bfloat16"),
+    "EQ": ("sbuf", [128, 512], "float8_e4m3fn_x4"), "ES": ("sbuf", [128, 512], "uint8"),
+    "A0B": ("sbuf", [128, 576], "bfloat16"),
+    "M": ("sbuf", [128, 1152], "bfloat16"), "RB": ("sbuf", [128, 1152], "bfloat16"), "SB": ("sbuf", [128, 1152], "bfloat16"),
+    "SR": ("sbuf", [128, 576], "float32"), "ERO": ("sbuf", [128, 576], "float32"), "SE": ("sbuf", [128, 576], "float32"),
+    "SY": ("sbuf", [128, 288], "float32"), "PP": ("sbuf", [128, 288], "float32"),
+    "WA": ("sbuf", [128, 288], "float32"), "WB": ("sbuf", [128, 288], "float32"),
+    "KR": ("sbuf", [128, 304], "float32"), "KC": ("sbuf", [128, 288], "float32"),
+    "EA": ("sbuf", [128, 56], "float32"), "DM": ("sbuf", [128, 56], "float32"), "LF": ("sbuf", [128, 56], "float32"),
+    "AB": ("sbuf", [128, 56], "float32"), "DP": ("sbuf", [128, 56], "float32"), "LU": ("sbuf", [128, 64], "uint16"),
+    "QS": ("sbuf", [128, 144], "float32"), "TU": ("sbuf", [128, 96], "uint16"), "YW": ("sbuf", [128, 32], "uint16"),
+    "YG": ("sbuf", [128, 288], "float32"), "YF": ("sbuf", [128, 288], "float32"),
+    "PLB": ("sbuf", [128, 576], "float32"), "YO": ("sbuf", [128, 288], "float32"),
+    "PS": ("psum", [128, 4096], "float32"),
+}
+for _r in range(4):
+    SCRATCH["X%d" % _r] = ("sbuf", [128, 1152], "bfloat16")
+    SCRATCH["XQ%d" % _r] = ("sbuf", [128, 288], "float8_e4m3fn_x4")
+    SCRATCH["XS%d" % _r] = ("sbuf", [128, 288], "uint8")
+for _r in range(3):
+    for _name, _w, _d in (("V", 1152, "bfloat16"), ("VC", 1152, "bfloat16"), ("Z", 1152, "bfloat16"), ("H", 1152, "bfloat16"),
+                          ("HP", 576, "bfloat16"), ("XP", 1152, "bfloat16"),
+                          ("ZQ", 288, "float8_e4m3fn_x4"), ("ZS", 288, "uint8"), ("HQ", 144, "float8_e4m3fn_x4"),
+                          ("HS", 144, "uint8"), ("HL", 144, "float8_e4m3fn_x4"), ("HM", 144, "uint8"),
+                          ("KS", 16, "uint16"), ("KL", 16, "uint16"), ("KO", 16, "uint16"), ("LP", 32, "uint16"),
+                          ("AU", 64, "uint16"), ("ROW", 576, "float32"), ("YR", 288, "float32")):
+        SCRATCH["%s%d" % (_name, _r)] = ("sbuf", [128, _w], _d)
+
+SEMAPHORES = ["cV", "cS", "cT", "cG", "out", "rl"] + ["ld%d" % i for i in range(12)] + \
+    ["a%s%d" % (k, r) for k in ("k", "p", "c", "s") for r in range(3)]
+
+
+def rank_program(g, core, T, topo):
+    rank = T.rank_of(core)
+    if rank is None:
+        return
+    eng = {"V": g.vector, "S": g.scalar, "T": g.tensor, "G": g, "Y": g.sync}
+    csem = {"V": "cV", "S": "cS", "T": "cT", "G": "cG"}
+    count = {"cV": 0, "cS": 0, "cT": 0, "cG": 0, "out": 0, "rl": 0}
+    know = {q: {} for q in eng}
+    uses = {}
+    order = [0]
+
+    def A(name, lo, hi, ph=None):
+        ap = T[name][:, lo:hi] if ph is None else T[name][:, lo + ph:hi:4]
+        return ap, [(name, lo, hi, ph)]
+
+    def CF(name, w=18, lo=0):
+        return A("CF", _F[name] + lo, _F[name] + lo + w)
+
+    def LI(name, w=18):
+        return A("LI", _L[name], _L[name] + w)
+
+    def CU(name, w=18, lo=0):
+        return A("CU", _U[name] + lo, _U[name] + lo + w)
+
+    def E16(name, lo, hi):
+        return T[name][:, lo + 15:hi:16], [(name, lo, hi, None)]
+
+    def B8(name, lo, hi):
+        return T[name][:, lo:hi].bitcast(dt.uint8), [(name, lo, hi, None)]
+
+    def ind(win, off):
+        return win[0].indirect(off[0]), win[1] + off[1]
+
+    def BANK(i, n):
+        return T["PS"][:, 512 * i:512 * i + n], [("PS", i, i + 1, None)]
+
+    def deps(q, ins, outs):
+        found = {}
+        for regs, w in ((ins, False), (outs, True)):
+            for (name, lo, hi, ph) in regs:
+                for (l2, h2, p2, w2, op) in uses.get(name, ()):
+                    if hi <= l2 or h2 <= lo or not (ph is None or p2 is None or ph == p2):
+                        continue
+                    same = op["q"] == q and op["compute"]
+                    if name == "PS":
+                        if same:
+                            continue
+                    elif not (w or w2) or (same and w and not w2):
+                        continue
+                    found[op["n"]] = op
+        for n in sorted(found, reverse=True):
+            op = found[n]
+            if know[q].get(op["sem"], 0) < op["val"]:
+                eng[q].wait_ge(T.sem[op["sem"]], op["val"])
+                know[q][op["sem"]] = op["val"]
+                for s, v in op["know"].items():
+                    if know[q].get(s, 0) < v:
+                        know[q][s] = v
+
+    def note(op, ins, outs):
+        order[0] += 1
+        op["n"] = order[0]
+        for regs, w in ((ins, False), (outs, True)):
+            for (name, lo, hi, ph) in regs:
+                uses.setdefault(name, []).append((lo, hi, ph, w, op))
+
+    def regs_of(args):
+        out = []
+        for a in args:
+            out += a[1]
+        return out
+
+    def emit(q, fn, outs, ins):
+        ri, ro = regs_of(ins), regs_of(outs)
+        deps(q, ri, ro)
+        s = csem[q]
+        count[s] += 1
+        fn(eng[q]).then_inc(T.sem[s], 1)
+        note({"q": q, "compute": True, "sem": s, "val": count[s], "know": dict(know[q])}, ri, ro)
+
+    def load(q, sem, dst, src):
+        deps(q, [], dst[1])
+        eng[q].dma_start(dst[0], src).then_inc(T.sem[sem], 16)
+        note({"q": q, "compute": False, "sem": sem, "val": 16, "know": dict(know[q])}, [], dst[1])
+
+    def store(q, dst, src):
+        deps(q, src[1], [])
+        eng[q].dma_start(dst, src[0]).then_inc(T.sem.out, 16)
+        count["out"] += 16
+
+    def send(to, dst, src, sem):
+        c = T.cores[to]
+        deps("G", src[1], [])
+        rid, pid = topo.addr(c, core)
+        n = len(topo.engines(core, c))
+        g.remote_dma(dst[0], src[0], T.sem[sem], T.sem.rl, pid, rid, topo.mask(core, c))
+        count["rl"] += n
+        note({"q": "G", "compute": False, "sem": sem, "val": n, "know": {}}, [], dst[1])
+
+    def sc(a):
+        return a[0] if isinstance(a, tuple) else a
+
+    def more(*a):
+        return [b for b in a if isinstance(b, tuple)]
+
+    def ts(out, in0, s1, s2, op0, op1=None):
+        if op1 is None:
+            emit("V", lambda e: e.tensor_scalar(out[0], in0[0], sc(s1), None, op0), [out], [in0] + more(s1))
+        else:
+            emit("V", lambda e: e.tensor_scalar(out[0], in0[0], sc(s1), sc(s2), op0, op1), [out], [in0] + more(s1, s2))
+
+    def tt(out, a, b, op):
+        emit("V", lambda e: e.tensor_tensor(out[0], a[0], b[0], op), [out], [a, b])
+
+    def cp(out, a):
+        emit("V", lambda e: e.tensor_copy(out[0], a[0]), [out], [a])
+
+    def act(out, a, f=Act.Copy, scale=1.0):
+        emit("S", lambda e: e.activation(out[0], a[0], f, scale=scale), [out], [a])
+
+    def move(q, out, a):
+        if q == "V":
+            cp(out, a)
+        else:
+            act(out, a)
+
+    def scan(out, data, n, bits=False):
+        d0 = A("A0B", 0, n) if bits else CF("A0", n)
+        emit("V", lambda e: e.tensor_tensor_scan(out[0], d0[0], data[0], 0.0, Op.mult, Op.add), [out], [d0, data])
+
+    def quant(qn, sn, lo, hi, src):
+        a, b = A(qn, lo, hi), A(sn, lo, hi)
+        emit("V", lambda e: e.quantize_mx(a[0], b[0], src[0]), [a, b], [src])
+
+    def mm(bank, wn, sn, wlo, xn, pn, lo, hi):
+        o = BANK(bank, hi - lo)
+        ins = [A(wn, wlo, wlo + 128), A(sn, wlo, wlo + 128), A(xn, lo, hi), A(pn, lo, hi)]
+        emit("T", lambda e: e.matmul_mx(o[0], ins[0][0], ins[1][0], ins[2][0], ins[3][0], True, True), [o], ins)
+
+    def iota(out, pattern, base, mult, f32):
+        if f32:
+            emit("G", lambda e: e.iota(out[0], pattern, base, mult, allow_small_or_imprecise_dtypes=True), [out], [])
+        else:
+            emit("G", lambda e: e.iota(out[0], pattern, base, mult), [out], [])
+
+    def planar(r, a, b):
+        for t in range(4):
+            o, i = A("XP%d" % r, 288 * t + a, 288 * t + b), A("X%d" % r, 4 * a, 4 * b, t)
+            emit("G", lambda e: e.affine_select(o[0], i[0], [[0, b - a]], Op.is_gt, 0.0, 1, 0), [o], [i])
+
+    def value(out, sc_name, lo, hi):
+        ts(out, E16(sc_name, lo, hi), CF("INV", 1), 0.25, Op.mult, Op.add)
+
+    def chain(out, lo, win, off, o0, split=True):
+        if split == "V":
+            cp(A(out, lo, lo + 288), ind(win, A(off, o0, o0 + 18)))
+        elif split:
+            cp(A(out, lo, lo + 160), ind(win, A(off, o0, o0 + 10)))
+            act(A(out, lo + 160, lo + 288), ind(win, A(off, o0 + 10, o0 + 18)))
+        else:
+            act(A(out, lo, lo + 288), ind(win, A(off, o0, o0 + 18)))
+
+    load("Y", "ld0", LI("pb"), T.pb[:, :])
+    load("S", "ld1", A("ut", 0, 512), T.u[:, :])
+    load("Y", "ld4", A("X0", 0, 1152), T.x[:, :])
+    load("S", "ld5", LI("lg"), T.lg[:, :])
+    load("S", "ld3", LI("fd"), T.fd[:, :])
+    load("Y", "ld2", LI("ex"), T.ex[:, :])
+    load("Y", "ld6", B8("wq", 0, 512), T.wc[:, :])
+    load("Y", "ld7", A("wp", 0, 512), T.ws[:, :])
+    load("Y", "ld8", A("vt", 0, 512), T.v[:, :])
+
+    iota(LI("PI", 1), [[0, 1]], 0, 1, False)
+    iota(CF("TM", 288), [[0, 18], [1, 16]], 0, 0, True)
+    iota(CF("IOT", 288), [[1, 288]], 0, 0, True)
+    iota(LI("UL", 32), [[1, 4], [16, 8]], 0, 0, False)
+    iota(CF("KW"), [[16, 18]], 0, 0, True)
+
+    emit("V", lambda e: e.memset(T.ONE[:, :], 1.0), [A("ONE", 0, 512)], [])
+    ts(LI("PM", 1), LI("PI", 1), 15, None, Op.bitwise_and)
+    cp(CF("PMF", 1), LI("PM", 1))
+    ts(CF("PM1", 1), CF("PMF", 1), 1.0, None, Op.add)
+    ts(CF("T15", 1), CF("PMF", 1), 15.0, 1.0 - 1.0 / K, Op.is_equal, Op.mult)
+    ts(CF("A1", 288), CF("TM", 288), CF("PMF", 1), 1.0, Op.subtract, Op.is_ge)
+    ts(CF("A2", 288), CF("TM", 288), CF("PM1", 1), K - 1.0, Op.is_equal, Op.mult)
+    ts(CF("INV", 1), CF("T15", 1), 1.0 / K, None, Op.add)
+    tt(CF("A0", 288), CF("A1", 288), CF("A2", 288), Op.add)
+    cp(A("AU0", 0, 18), LI("pb"))
+    send(rank ^ MASK[0], A("LP0", 0, 18), A("AU0", 0, 18), "ap0")
+    act(A("A0B", 0, 288), CF("A0", 288))
+    act(A("A0B", 288, 576), CF("A0", 288))
+    cp(CU("ULU", 32), LI("UL", 32))
+    ts(CF("CW"), CF("KW"), CF("PMF", 1), None, Op.add)
+    for i in range(3):
+        ts(A("AB", 18 * i, 18 * i + 18), CF("CW"), 0.25, None, Op.add)
+
+    planar(0, 0, C)
+
+    def onehot(b):
+        emit("G", lambda e: e.affine_select(T.ET[:, 512 * b:512 * b + 512], T.ONE[:, :], [[-1, 512]], Op.is_equal, 0.0, b, 4),
+             [A("ET", 512 * b, 512 * b + 512)], [A("ONE", 0, 512)])
+
+    for b in range(4):
+        onehot(b)
+
+    cp(CU("LGU"), LI("lg"))
+    cp(CU("FU"), LI("fd"))
+    chain("YR0", 0, CF("IOT", 288), "CU", _U["LGU"], False)
+    def stand(j, n):
+        off, o = CU("ULU", 8 * n, 8 * j), (128 * j, 128 * (j + n))
+        emit("V", lambda e: e.tensor_copy(T.uq2[:, o[0]:o[1]].bitcast(dt.uint32),
+                                          T.uq[:, 0:128].bitcast(dt.uint32).indirect(off[0])),
+             [A("uq2", o[0], o[1])], [A("uq", 0, 128), off])
+        emit("S", lambda e: e.activation(T.us2[:, o[0]:o[1]], T.us[:, 0:128].indirect(off[0]), Act.Copy),
+             [A("us2", o[0], o[1])], [A("us", 0, 128), off])
+
+    cp(CF("EXF"), LI("ex"))
+    quant("uq", "us", 0, 128, A("ut", 0, 512))
+    tt(CF("LOWF"), CF("EXF"), CF("CW"), Op.min)
+    tt(CF("D1"), CF("EXF"), CF("CW"), Op.subtract)
+    stand(1, 2)
+    cp(A("LU", 18, 36), CF("LOWF"))
+    quant("XQ0", "XS0", 0, 288, A("X0", 0, 1152))
+    chain("YG", 0, A("YR0", 0, 288), "CU", _U["FU"], False)
+    stand(0, 1)
+    stand(3, 1)
+    for j in (2, 1, 0, 3):
+        mm(j, "uq2", "us2", 128 * j, "XQ0", "XS0", 0, 288)
+    for i in range(3):
+        ts(A("DP", 18 * i, 18 * i + 18), CF("D1"), CF("INV", 1), None, Op.mult)
+
+    def msig(q, j, lo, hi):
+        o, i = A("M", 288 * j + lo, 288 * j + hi), BANK(j, hi - lo)
+        if q == "V":
+            ts(o, i, 0.0, None, Op.is_lt)
+        else:
+            act(o, i, Act.Sign, -1.0)
+
+    def rbit(q, j, lst):
+        s = SLOT[j]
+        o, i = A("RB", 288 * s, 288 * s + 288), ind(A("M", 288 * j, 288 * j + 288), lst)
+        if q == "V":
+            ts(o, i, 0.0, None, Op.max)
+        else:
+            act(o, i, Act.Relu)
+
+    def choose(s, n, at, between=()):
+        a, b = A("QS", 18 * s, 18 * (s + n)), A("QS", 72 + 18 * s, 72 + 18 * (s + n))
+        steps = [lambda: scan(A("SB", 288 * s, 288 * (s + n)), A("RB", 288 * s, 288 * (s + n)), 288 * n, bits=True),
+                 lambda: tt(a, E16("SB", 288 * s, 288 * (s + n)), A("DP", at, at + 18 * n), Op.mult),
+                 lambda: tt(b, a, A("AB", at, at + 18 * n), Op.add),
+                 lambda: cp(A("TU", 18 * s, 18 * (s + n)), b)]
+        for i, step in enumerate(steps):
+            step()
+            if i < len(between):
+                between[i]()
+
+    LOW = A("LU", 18, 36)
+
+    for r in range(3):
+        other = rank ^ MASK[r]
+        x, xn, last = "X%d" % r, "X%d" % (r + 1), r == 2
+        v, vc, z, h, hp = "V%d" % r, "VC%d" % r, "Z%d" % r, "H%d" % r, "HP%d" % r
+        ks, kl, ko, au, lp = "KS%d" % r, "KL%d" % r, "KO%d" % r, "AU%d" % r, "LP%d" % r
+        yn = "PLB" if last else "YR%d" % (r + 1)
+        yrow = A(yn, 0, 288)
+        pp = A("PP", 0, 288)
+        if r == 0:
+            msig("V", 2, 0, C)
+            msig("S", 1, 0, C)
+            chain("YF", 0, A("YG", 0, 288), "CU", _U["FU"], "V")
+            rbit("V", 2, LOW)
+            rbit("S", 1, LOW)
+            msig("S", 0, 0, C)
+            rbit("S", 0, LOW)
+            act(CF("FR", 288), ind(CF("IOT", 288), CU("FU")))
+            choose(0, 2, 0, (lambda: chain("ROW0", 288, A("YF", 0, 288), "CU", _U["FU"], "V"),
+                             lambda: scan(A("SR", 288, 576), A("ROW0", 288, 576), 288)))
+            choose(2, 1, 36, (lambda: chain("WA", 0, CF("IOT", 288), "TU", 0),
+                              lambda: value(A("AU0", 18, 36), "SR", 288, 576),
+                              lambda: chain("WB", 0, A("WA", 0, 288), "AU0", 0)))
+            chain("WA", 0, A("WB", 0, 288), "TU", 18)
+            chain("WB", 0, A("WA", 0, 288), lp, 0)
+            chain("WA", 0, A("WB", 0, 288), "TU", 36)
+            chain("YF", 0, A("WA", 0, 288), "AU0", 18)
+            chain("PP", 0, CF("IOT", 288), lp, 0, False)
+            scan(A("SY", 0, 288), A("YF", 0, 288), 288)
+            value(A("YW", 0, 18), "SY", 0, 288)
+            chain(yn, 0, pp, "YW", 0)
+        else:
+            msig("V", 2, 0, HALF)
+            msig("S", 1, 0, HALF)
+            rbit("V", 2, A("LU", 0, 18))
+            rbit("S", 1, LOW)
+            msig("S", 0, 0, HALF)
+            chain("PP", 0, CF("IOT", 288), lp, 0, False)
+            choose(0, 2, 0)
+            rbit("S", 0, A("LU", 36, 54))
+            chain("WA", 0, pp, "TU", 0)
+            choose(2, 1, 36)
+            chain("WB", 0, A("WA", 0, 288), "TU", 18, False)
+            chain("WA", 0, A("WB", 0, 288), lp, 0)
+            chain(yn, 0, A("WA", 0, 288), "TU", 36)
+        scan(A("SY", 0, 288), yrow, 288)
+        value(A("YW", 0, 18), "SY", 0, 288)
+
+        def gv(t):
+            act(A(v, 288 * t, 288 * t + 288), ind(A("XP%d" % r, 288 * t, 288 * t + 288), A("YW", 0, 18)), Act.Copy, 0.5)
+
+        def gz(t, a, b):
+            f = CU("FU") if (a, b) == (0, C) else CU("FH", 9, 10 * (a // HALF))
+            w = A(v, 288 * t, 288 * t + 288)
+            tt(A(z, 4 * a, 4 * b, t), ind(w, f), A(vc, 288 * t + a, 288 * t + b), Op.add)
+
+        def gc(q, t):
+            move(q, A(vc, 288 * t, 288 * t + 288), A(v, 288 * t, 288 * t + 288))
+
+        act(A("KR", 0, 144), ind(CF("FR", 288), A("YW", 0, 9)))
+        ts(A(v, 0, 288), ind(A("XP%d" % r, 0, 288), A("YW", 0, 18)), 0.5, None, Op.mult)
+        scan(A("KC", 0, 144), A("KR", 0, 144), 144)
+        gc("V", 0)
+        value(A(ks, 0, 9), "KC", 0, 144)
+        for t in (1, 2, 3):
+            gv(t)
+        gc("V", 1)
+        send(other, A(kl, 0, 9), A(ks, 0, 9), "ak%d" % r)
+        if r == 0:
+            cp(CU("FH", 9, 0), A("LI", _L["fd"], _L["fd"] + 9))
+            cp(CU("FH", 9, 10), A("LI", _L["fd"] + 9, _L["fd"] + 18))
+        for t in (2, 3):
+            gc("S", t)
+        msig("S", 3, 0, C if r == 0 else HALF)
+        rbit("S", 3, LOW)
+        act(A("KR", 144, 304), ind(CF("FR", 288), A("YW", 8, 18)))
+        zq, zs = "ZQ%d" % r, "ZS%d" % r
+        for t in (0, 1, 2):
+            gz(t, 0, C)
+        gz(3, 0, HALF)
+        quant(zq, zs, 0, HALF, A(z, 0, 576))
+        gz(3, HALF, C)
+        quant(zq, zs, HALF, C, A(z, 576, 1152))
+
+        def ev(q, hf, b):
+            o, i = A(h, 288 * b + 144 * hf, 288 * b + 144 * hf + 144), BANK(4 * hf + b, HALF)
+            if q == "V":
+                ts(o, i, 0.03125, None, Op.mult)
+            else:
+                act(o, i, Act.Copy, 0.03125)
+
+        for b in range(4):
+            mm(b, "wq", "wp", 128 * b, zq, zs, 0, HALF)
+            ev("S", 0, b)
+        for b in range(4):
+            mm(4 + b, "wq", "wp", 128 * b, zq, zs, HALF, C)
+            ev("S" if b < 2 else "V", 1, b)
+        for q, b, at, to in (("S", 0, 0, 9), ("V", 2, 0, 9), ("S", 1, 0, 9), ("V", 3, 0, 4), ("S", 3, 4, 9)):
+            move(q, A(hp, 64 * at, 64 * to, b), ind(A(h, 288 * b, 288 * b + 288), A(kl, at, to)))
+        hq, hs, hl, hm = "HQ%d" % r, "HS%d" % r, "HL%d" % r, "HM%d" % r
+        quant(hq, hs, 0, HALF, A(hp, 0, 576))
+        send(other, B8(hl, 0, HALF), B8(hq, 0, HALF), "ac%d" % r)
+        send(other, A(hm, 0, HALF), A(hs, 0, HALF), "as%d" % r)
+        def own(b):
+            tt(A(xn, 576, 1152, b), ind(A(h, 288 * b, 288 * b + 288), A(ko, 0, 9)), A(x, 576, 1152, b), Op.add)
+
+        nr = r + 1
+        xq, xs = "XQ%d" % nr, "XS%d" % nr
+        rown, aun = ("PLB" if last else "ROW%d" % nr), "AU%d" % nr
+        plo = 288 if last else 0
+        prow_old = A("ROW%d" % r, 0, 288)
+        if r == 0:
+            act(prow_old, ind(CF("IOT", 288), A("AU0", 0, 18)))
+        if not last:
+            chain("YG", 0, yrow, "CU", _U["FU"], False)
+        choose(3, 1, 18, (lambda: scan(A("KC", 144, 288), A("KR", 160, 304), 144),
+                          lambda: value(A(ko, 0, 9), "KC", 144, 288), lambda: own(0)))
+        act(A(rown, plo, plo + 288), ind(prow_old, A("TU", 54, 72)))
+        if last:
+            store("Y", T.pl[:, :], (T.PLB[0:128:16, :], [("PLB", 0, 576, None)]))
+            for b in (1, 2, 3):
+                own(b)
+            quant(xq, xs, HALF, C, A(xn, 576, 1152))
+            quant("vq", "vs", 0, 128, A("vt", 0, 512))
+        else:
+            own(1)
+            if r == 0:
+                cp(CU("EXU"), LI("ex"))
+                ts(A("EA", 18, 36), CF("EXF"), 0.25, None, Op.add)
+            chain("YF", 0, A("YG", 0, 288), "CU", _U["FU"], False)
+            chain(rown, 288, A("YF", 0, 288), "CU", _U["FU"], False)
+            own(2)
+            own(3)
+            scan(A("SR", 0, 288), A(rown, 0, 288), 288)
+            quant(xq, xs, HALF, C, A(xn, 576, 1152))
+            value(A("AB", 0, 18), "SR", 0, 288)
+            scan(A("SR", 288, 576), A(rown, 288, 576), 288)
+            cp(A(aun, 0, 18), A("AB", 0, 18))
+            send(rank ^ MASK[nr], A("LP%d" % nr, 0, 18), A(aun, 0, 18), "ap%d" % nr)
+            planar(nr, HALF, C)
+            if r == 0:
+                act(CF("ER", 288), ind(CF("IOT", 288), CU("EXU")))
+            act(A("ERO", 0, 288), ind(CF("ER", 288), A(aun, 0, 18)))
+            value(A("AB", 36, 54), "SR", 288, 576)
+            cp(A(aun, 18, 36), A("AB", 36, 54))
+            act(A("ERO", 288, 576), ind(CF("ER", 288), A(aun, 18, 36)))
+            for j in (2, 1, 0, 3):
+                mm(j, "uq2", "us2", 128 * j, xq, xs, HALF, C)
+                msig("S", j, HALF, C)
+            if r == 0:
+                quant("EQ", "ES", 0, 512, A("ET", 0, 2048))
+            for i, at in ((0, 0), (1, 36)):
+                scan(A("SE", 288 * i, 288 * i + 288), A("ERO", 288 * i, 288 * i + 288), 288)
+                value(A("EA", at, at + 18), "SE", 288 * i, 288 * i + 288)
+
+        def yout(a, b, bank):
+            mm(bank, "vq", "vs", 0, xq, xs, a, b)
+            act(A("YO", a, b), BANK(bank, b - a))
+
+        def osc(q, k, a, b):
+            store(q, T.osc[4 * k:4 * k + 4, a:b], (T[xs][32 * k:32 * k + 4, a:b], [(xs, a, b, None)]))
+
+        def stores(a, b):
+            yout(a, b, a // HALF)
+            store("Y", T.oc[:, 4 * a:4 * b], B8(xq, a, b))
+            store("S", T.y[:, a:b], A("YO", a, b))
+            for k in range(4):
+                osc("Y" if k < 3 else "S", k, a, b)
+
+        if last:
+            stores(HALF, C)
+        for b in range(4):
+            mm(4 + b, "EQ", "ES", 128 * b, hl, hm, 0, HALF)
+            tt(A(xn, 0, 576, b), A(x, 0, 576, b), BANK(4 + b, HALF), Op.add)
+        quant(xq, xs, 0, HALF, A(xn, 0, 576))
+        if last:
+            stores(0, HALF)
+        else:
+            planar(nr, 0, HALF)
+            tt(A("LF", 0, 54), A("EA", 0, 54), A("AB", 0, 54), Op.min)
+            tt(A("DM", 0, 54), A("EA", 0, 54), A("AB", 0, 54), Op.subtract)
+            cp(A("LU", 0, 54), A("LF", 0, 54))
+            ts(A("DP", 0, 54), A("DM", 0, 54), CF("INV", 1), None, Op.mult)
+            for j in (2, 1, 0, 3):
+                mm(j, "uq2", "us2", 128 * j, xq, xs, 0, HALF)
+    for s in ("cV", "cS", "cT", "cG", "out", "rl"):
+        g.wait_ge(T.sem[s], count[s])

@@ -1,38 +1,43 @@
-from concourse.mybir import dt, AluOpType as Op, ActivationFunctionType as Act
+from concourse.mybir import dt, AluOpType as Op, ActivationFunctionType as Act, AxisListType as Ax
 
 C, HALF = 288, 144
 MASK = [4, 1, 2]
-K = 65536.0
-SLOT = {2: 0, 1: 1, 0: 2, 3: 3}
+K16, K4, PACK = 2.0 ** 30, 2.0 ** 28, 16384.0
+ZCUT = (0, 20, 40, 56, 72)
+ZMID = 160
 _F = {}
 _n = 0
-for _name, _w in (("TM", 288), ("A1", 288), ("A2", 288), ("A0", 288), ("IOT", 288), ("ER", 288), ("FR", 288), ("FF", 288),
-                  ("F3", 288), ("F3S", 288), ("KW", 24), ("CW", 24), ("EXF", 24), ("LOWF", 24), ("D1", 24),
-                  ("PMF", 8), ("PM1", 8), ("T15", 8), ("INV", 8)):
+for _name, _w in (("IOT", 288), ("IOB", 288), ("PK", 288), ("KW", 24), ("CW", 24), ("CX", 32), ("CY", 32), ("LX", 32),
+                  ("UW", 8), ("TM4", 16), ("S1", 16), ("S2", 16), ("S3", 8), ("COL", 8), ("TMP", 24), ("SG", 24),
+                  ("PM1", 1), ("MSK", 1), ("NMS", 1), ("HA", 1), ("HB", 1), ("GO", 1), ("I16", 1), ("I4", 1),
+                  ("I4Y", 1), ("I4F", 1), ("TA", 1), ("TB", 1)):
     _F[_name] = _n
     _n += _w
-_L = {"pb": 0, "ex": 24, "fd": 48, "lg": 72, "PI": 96, "PM": 104, "UL": 112}
-_U = {"FU": 0, "F3U": 32, "EXU": 64, "LGU": 96, "FH": 160, "ULU": 192}
+_COL = {"PM": (0, 15), "P4": (2, 3), "T4": (0, 3), "H": (4, 1), "O": (0, 1), "P32": (0, 31)}
+_L = {"pb": 0, "fd": 24, "lg": 48}
+_U = {"FU": 0, "F3U": 32, "EXU": 64, "LGU": 96, "PML": 128, "UL": 160, "GL": 176, "L": 192}
+UP, EX, DN = 8, 32, 56
 
 SCRATCH = {
-    "CF": ("sbuf", [128, _n], "float32"), "LI": ("sbuf", [128, 144], "int32"), "CU": ("sbuf", [128, 224], "uint16"),
+    "CF": ("sbuf", [128, _n], "float32"), "LI": ("sbuf", [128, 72], "int32"), "CU": ("sbuf", [128, 224], "uint16"),
+    "PI": ("sbuf", [128, 16], "int32"), "EXW": ("sbuf", [128, 96], "int32"), "KI": ("sbuf", [128, 144], "int32"),
     "ut": ("sbuf", [128, 512], "bfloat16"), "vt": ("sbuf", [128, 512], "bfloat16"),
     "uq": ("sbuf", [128, 128], "float8_e4m3fn_x4"), "us": ("sbuf", [128, 128], "uint8"),
-    "uq2": ("sbuf", [128, 512], "float8_e4m3fn_x4"), "us2": ("sbuf", [128, 512], "uint8"),
+    "uq2": ("sbuf", [128, 128], "float8_e4m3fn_x4"), "us2": ("sbuf", [128, 128], "uint8"),
     "vq": ("sbuf", [128, 128], "float8_e4m3fn_x4"), "vs": ("sbuf", [128, 128], "uint8"),
     "wq": ("sbuf", [128, 512], "float8_e4m3fn_x4"), "wp": ("sbuf", [128, 512], "uint8"),
     "ONE": ("sbuf", [128, 512], "bfloat16"), "ET": ("sbuf", [128, 2048], "bfloat16"),
     "EQ": ("sbuf", [128, 512], "float8_e4m3fn_x4"), "ES": ("sbuf", [128, 512], "uint8"),
-    "A0B": ("sbuf", [128, 576], "bfloat16"),
-    "M": ("sbuf", [128, 1152], "bfloat16"), "RB": ("sbuf", [128, 1152], "bfloat16"), "SB": ("sbuf", [128, 1152], "bfloat16"),
-    "SR": ("sbuf", [128, 576], "float32"), "ERO": ("sbuf", [128, 576], "float32"), "SE": ("sbuf", [128, 576], "float32"),
+    "PAT": ("sbuf", [128, 32], "bfloat16"), "D16": ("sbuf", [128, 288], "bfloat16"), "D4": ("sbuf", [128, 288], "bfloat16"),
+    "M": ("sbuf", [128, 576], "bfloat16"), "RB": ("sbuf", [128, 288], "bfloat16"), "TR": ("sbuf", [128, 320], "bfloat16"),
+    "RA": ("sbuf", [128, 288], "bfloat16"), "RE": ("sbuf", [128, 288], "bfloat16"), "RF": ("sbuf", [128, 288], "bfloat16"),
+    "SA": ("sbuf", [128, 288], "bfloat16"), "SE": ("sbuf", [128, 288], "bfloat16"), "SF": ("sbuf", [128, 288], "bfloat16"),
     "SY": ("sbuf", [128, 288], "float32"), "PP": ("sbuf", [128, 288], "float32"),
-    "WA": ("sbuf", [128, 288], "float32"), "WB": ("sbuf", [128, 288], "float32"),
-    "KR": ("sbuf", [128, 304], "float32"), "KC": ("sbuf", [128, 288], "float32"),
-    "EA": ("sbuf", [128, 56], "float32"), "DM": ("sbuf", [128, 56], "float32"), "LF": ("sbuf", [128, 56], "float32"),
-    "AB": ("sbuf", [128, 56], "float32"), "DP": ("sbuf", [128, 56], "float32"), "LU": ("sbuf", [128, 64], "uint16"),
-    "QS": ("sbuf", [128, 144], "float32"), "TU": ("sbuf", [128, 96], "uint16"), "YW": ("sbuf", [128, 32], "uint16"),
-    "YG": ("sbuf", [128, 288], "float32"), "YF": ("sbuf", [128, 288], "float32"),
+    "WA": ("sbuf", [128, 288], "float32"), "WB": ("sbuf", [128, 288], "float32"), "WC": ("sbuf", [128, 288], "float32"),
+    "YR": ("sbuf", [128, 288], "float32"), "QC": ("sbuf", [128, 36], "float32"), "QP": ("sbuf", [128, 36], "float32"),
+    "QS": ("sbuf", [128, 108], "float32"), "TU": ("sbuf", [128, 54], "uint16"), "AL": ("sbuf", [128, 18], "uint16"),
+    "Y4": ("sbuf", [128, 72], "uint16"), "YF4": ("sbuf", [128, 72], "uint16"),
+    "XH": ("sbuf", [128, 1152], "bfloat16"), "V": ("sbuf", [128, 1152], "bfloat16"),
     "PLB": ("sbuf", [128, 576], "float32"), "YO": ("sbuf", [128, 288], "float32"),
     "PS": ("psum", [128, 4096], "float32"),
 }
@@ -40,13 +45,13 @@ for _r in range(4):
     SCRATCH["X%d" % _r] = ("sbuf", [128, 1152], "bfloat16")
     SCRATCH["XQ%d" % _r] = ("sbuf", [128, 288], "float8_e4m3fn_x4")
     SCRATCH["XS%d" % _r] = ("sbuf", [128, 288], "uint8")
+    SCRATCH["QO%d" % _r] = ("sbuf", [128, 36], "float32")
+    SCRATCH["AU%d" % _r] = ("sbuf", [128, 18], "uint16")
 for _r in range(3):
-    for _name, _w, _d in (("V", 1152, "bfloat16"), ("VC", 1152, "bfloat16"), ("Z", 1152, "bfloat16"), ("H", 1152, "bfloat16"),
-                          ("HP", 576, "bfloat16"), ("XP", 1152, "bfloat16"),
+    for _name, _w, _d in (("Z", 1152, "bfloat16"), ("H", 1152, "bfloat16"), ("HP", 576, "bfloat16"),
                           ("ZQ", 288, "float8_e4m3fn_x4"), ("ZS", 288, "uint8"), ("HQ", 144, "float8_e4m3fn_x4"),
                           ("HS", 144, "uint8"), ("HL", 144, "float8_e4m3fn_x4"), ("HM", 144, "uint8"),
-                          ("KS", 16, "uint16"), ("KL", 16, "uint16"), ("KO", 16, "uint16"), ("LP", 32, "uint16"),
-                          ("AU", 64, "uint16"), ("ROW", 576, "float32"), ("YR", 288, "float32")):
+                          ("KS", 72, "uint16"), ("KL", 36, "uint16"), ("LP", 18, "uint16")):
         SCRATCH["%s%d" % (_name, _r)] = ("sbuf", [128, _w], _d)
 
 SEMAPHORES = ["cV", "cS", "cT", "cG", "out", "rl"] + ["ld%d" % i for i in range(12)] + \
@@ -64,37 +69,36 @@ def rank_program(g, core, T, topo):
     uses = {}
     order = [0]
 
-    def A(name, lo, hi, ph=None):
-        ap = T[name][:, lo:hi] if ph is None else T[name][:, lo + ph:hi:4]
-        return ap, [(name, lo, hi, ph)]
+    def A(name, lo, hi, step=1):
+        return (T[name][:, lo:hi] if step == 1 else T[name][:, lo:hi:step]), [(name, lo, hi, step)]
 
-    def CF(name, w=18, lo=0):
+    def CF(name, w=1, lo=0):
         return A("CF", _F[name] + lo, _F[name] + lo + w)
 
-    def LI(name, w=18):
-        return A("LI", _L[name], _L[name] + w)
+    def COL(name):
+        return CF("COL", 1, list(_COL).index(name))
 
-    def CU(name, w=18, lo=0):
-        return A("CU", _U[name] + lo, _U[name] + lo + w)
+    def LI(name):
+        return A("LI", _L[name], _L[name] + 18)
 
-    def E16(name, lo, hi):
-        return T[name][:, lo + 15:hi:16], [(name, lo, hi, None)]
+    def CU(name, w=18, lo=0, step=1):
+        return A("CU", _U[name] + lo, _U[name] + w, step)
 
     def B8(name, lo, hi):
-        return T[name][:, lo:hi].bitcast(dt.uint8), [(name, lo, hi, None)]
+        return T[name][:, lo:hi].bitcast(dt.uint8), [(name, lo, hi, 1)]
 
     def ind(win, off):
         return win[0].indirect(off[0]), win[1] + off[1]
 
     def BANK(i, n):
-        return T["PS"][:, 512 * i:512 * i + n], [("PS", i, i + 1, None)]
+        return T["PS"][:, 512 * i:512 * i + n], [("PS", i, i + 1, 1)]
 
     def deps(q, ins, outs):
         found = {}
         for regs, w in ((ins, False), (outs, True)):
-            for (name, lo, hi, ph) in regs:
-                for (l2, h2, p2, w2, op) in uses.get(name, ()):
-                    if hi <= l2 or h2 <= lo or not (ph is None or p2 is None or ph == p2):
+            for (name, lo, hi, st) in regs:
+                for (l2, h2, s2, w2, op) in uses.get(name, ()):
+                    if hi <= l2 or h2 <= lo or (st == s2 and (lo - l2) % st):
                         continue
                     same = op["q"] == q and op["compute"]
                     if name == "PS":
@@ -116,8 +120,8 @@ def rank_program(g, core, T, topo):
         order[0] += 1
         op["n"] = order[0]
         for regs, w in ((ins, False), (outs, True)):
-            for (name, lo, hi, ph) in regs:
-                uses.setdefault(name, []).append((lo, hi, ph, w, op))
+            for (name, lo, hi, st) in regs:
+                uses.setdefault(name, []).append((lo, hi, st, w, op))
 
     def regs_of(args):
         out = []
@@ -170,18 +174,17 @@ def rank_program(g, core, T, topo):
     def cp(out, a):
         emit("V", lambda e: e.tensor_copy(out[0], a[0]), [out], [a])
 
-    def act(out, a, f=Act.Copy, scale=1.0):
-        emit("S", lambda e: e.activation(out[0], a[0], f, scale=scale), [out], [a])
+    def fill(out, c):
+        emit("V", lambda e: e.memset(out[0], c), [out], [])
 
-    def move(q, out, a):
-        if q == "V":
-            cp(out, a)
+    def act(out, a, f=Act.Copy, scale=1.0, bias=None):
+        if bias is None:
+            emit("S", lambda e: e.activation(out[0], a[0], f, scale=sc(scale)), [out], [a] + more(scale))
         else:
-            act(out, a)
+            emit("S", lambda e: e.activation(out[0], a[0], Act.Identity, bias=bias, scale=scale), [out], [a])
 
-    def scan(out, data, n, bits=False):
-        d0 = A("A0B", 0, n) if bits else CF("A0", n)
-        emit("V", lambda e: e.tensor_tensor_scan(out[0], d0[0], data[0], 0.0, Op.mult, Op.add), [out], [d0, data])
+    def scan(out, d0, d1):
+        emit("V", lambda e: e.tensor_tensor_scan(out[0], d0[0], d1[0], 0.0, Op.mult, Op.add), [out], [d0, d1])
 
     def quant(qn, sn, lo, hi, src):
         a, b = A(qn, lo, hi), A(sn, lo, hi)
@@ -192,309 +195,253 @@ def rank_program(g, core, T, topo):
         ins = [A(wn, wlo, wlo + 128), A(sn, wlo, wlo + 128), A(xn, lo, hi), A(pn, lo, hi)]
         emit("T", lambda e: e.matmul_mx(o[0], ins[0][0], ins[1][0], ins[2][0], ins[3][0], True, True), [o], ins)
 
-    def iota(out, pattern, base, mult, f32):
-        if f32:
-            emit("G", lambda e: e.iota(out[0], pattern, base, mult, allow_small_or_imprecise_dtypes=True), [out], [])
-        else:
-            emit("G", lambda e: e.iota(out[0], pattern, base, mult), [out], [])
+    def iota(out, pattern, base):
+        emit("G", lambda e: e.iota(out[0], pattern, base, 0, allow_small_or_imprecise_dtypes=True), [out], [])
 
-    def planar(r, a, b):
-        for t in range(4):
-            o, i = A("XP%d" % r, 288 * t + a, 288 * t + b), A("X%d" % r, 4 * a, 4 * b, t)
-            emit("G", lambda e: e.affine_select(o[0], i[0], [[0, b - a]], Op.is_gt, 0.0, 1, 0), [o], [i])
+    def row(name):
+        return A(name, 0, C)
 
-    def value(out, sc_name, lo, hi):
-        ts(out, E16(sc_name, lo, hi), CF("INV", 1), 0.25, Op.mult, Op.add)
+    def step(out, win, off):
+        name, lo = off[1][0][0], off[1][0][1]
+        cp(A(out, 0, 160), ind(win, A(name, lo, lo + 10)))
+        act(A(out, 160, C), ind(win, A(name, lo + 10, lo + 18)))
 
-    def chain(out, lo, win, off, o0, split=True):
-        if split == "V":
-            cp(A(out, lo, lo + 288), ind(win, A(off, o0, o0 + 18)))
-        elif split:
-            cp(A(out, lo, lo + 160), ind(win, A(off, o0, o0 + 10)))
-            act(A(out, lo + 160, lo + 288), ind(win, A(off, o0 + 10, o0 + 18)))
-        else:
-            act(A(out, lo, lo + 288), ind(win, A(off, o0, o0 + 18)))
+    def small(out, win, off, scale=1.0):
+        act(row(out), ind(win, off), None, scale, -float(HALF))
 
+    def wrap(out, a):
+        scan(row(out), row("D16"), row(a))
+
+    def value(out, a):
+        ts(out, A(a, 15, C, 16), CF("I16"), HALF + 0.25, Op.mult, Op.add)
+
+    fill(A("EXW", 0, 96), 0)
     load("Y", "ld0", LI("pb"), T.pb[:, :])
+    load("S", "ld3", LI("fd"), T.fd[:, :])
     load("S", "ld1", A("ut", 0, 512), T.u[:, :])
     load("Y", "ld4", A("X0", 0, 1152), T.x[:, :])
-    load("S", "ld5", LI("lg"), T.lg[:, :])
-    load("S", "ld3", LI("fd"), T.fd[:, :])
-    load("Y", "ld2", LI("ex"), T.ex[:, :])
+    load("S", "ld2", A("EXW", EX, EX + 18), T.ex[:, :])
+    load("Y", "ld9", (T.EXW[0:112, UP:UP + 18], [("EXW", UP, UP + 18, 1)]), T.ex[16:128, :])
+    load("S", "ld10", (T.EXW[16:128, DN:DN + 18], [("EXW", DN, DN + 18, 1)]), T.ex[0:112, :])
+    load("Y", "ld5", LI("lg"), T.lg[:, :])
     load("Y", "ld6", B8("wq", 0, 512), T.wc[:, :])
     load("Y", "ld7", A("wp", 0, 512), T.ws[:, :])
     load("Y", "ld8", A("vt", 0, 512), T.v[:, :])
 
-    iota(LI("PI", 1), [[0, 1]], 0, 1, False)
-    iota(CF("TM", 288), [[0, 18], [1, 16]], 0, 0, True)
-    iota(CF("IOT", 288), [[1, 288]], 0, 0, True)
-    iota(LI("UL", 32), [[1, 4], [16, 8]], 0, 0, False)
-    iota(CF("KW"), [[16, 18]], 0, 0, True)
+    emit("G", lambda e: e.iota(T.PI[:, 0:1], [[0, 1]], 0, 1), [A("PI", 0, 1)], [])
+    iota(CF("KW", 18), [[16, 18]], 0)
+    iota(CF("TM4", 16), [[0, 4], [1, 4]], 0)
+    iota(CF("IOT", C), [[1, C]], 0)
+    iota(CF("UW", 8), [[32, 4], [-16, 2]], 16)
+    iota(CF("CX", 32), [[32, 16], [0, 2]], 0)
 
-    emit("V", lambda e: e.memset(T.ONE[:, :], 1.0), [A("ONE", 0, 512)], [])
-    ts(LI("PM", 1), LI("PI", 1), 15, None, Op.bitwise_and)
-    cp(CF("PMF", 1), LI("PM", 1))
-    ts(CF("PM1", 1), CF("PMF", 1), 1.0, None, Op.add)
-    ts(CF("T15", 1), CF("PMF", 1), 15.0, 1.0 - 1.0 / K, Op.is_equal, Op.mult)
-    ts(CF("A1", 288), CF("TM", 288), CF("PMF", 1), 1.0, Op.subtract, Op.is_ge)
-    ts(CF("A2", 288), CF("TM", 288), CF("PM1", 1), K - 1.0, Op.is_equal, Op.mult)
-    ts(CF("INV", 1), CF("T15", 1), 1.0 / K, None, Op.add)
-    tt(CF("A0", 288), CF("A1", 288), CF("A2", 288), Op.add)
+    fill(A("ONE", 0, 512), 1.0)
+    fill(A("TR", 0, 32), 0.0)
+    for i, (a, b) in enumerate(_COL.values()):
+        ts(A("PI", 8 + i, 9 + i), A("PI", 0, 1), a, b, Op.logical_shift_right, Op.bitwise_and)
+    cp(CF("COL", 6), A("PI", 8, 14))
+    ts(CF("PM1"), COL("PM"), 1.0, None, Op.add)
+    ts(CU("PML"), CF("KW", 18), 0.0, COL("PM"), Op.mult, Op.add)
+    ts(CF("CW", 18), CF("KW", 18), COL("PM"), None, Op.add)
+    ts(A("PAT", 16, 32), CF("TM4", 16), COL("P4"), K4, Op.is_gt, Op.mult)
+    ts(CF("S3", 4), CF("TM4", 4), COL("P4"), 1.0 / K4, Op.is_le, Op.max)
+    ts(CF("GO"), COL("H"), COL("O"), DN - EX + 1.0, Op.subtract, Op.mult)
+    ts(CF("S1", 16), CF("IOT", 16), COL("PM"), None, Op.is_gt)
+    ts(CF("S2", 16), CF("IOT", 16), CF("PM1"), K16, Op.is_equal, Op.mult)
+    emit("V", lambda e: e.tensor_reduce(CF("I4")[0], CF("S3", 4)[0], Ax.X, Op.mult), [CF("I4")], [CF("S3", 4)])
+    act(row("D4"), ind(A("PAT", 16, 32), CU("PML")))
+    act(CF("IOB", C), CF("IOT", C), Act.Copy, PACK)
+    ts(CU("GL", 2), CF("CW", 2), CF("GO"), float(EX), Op.add, Op.add)
+    tt(A("PAT", 0, 16), CF("S1", 16), CF("S2", 16), Op.max)
+    ts(CF("I16"), COL("PM"), 15.0, 1.0 / K16, Op.is_equal, Op.max)
+    ts(CF("MSK"), COL("PM"), 8.0, None, Op.is_lt)
+    ts(CF("NMS"), COL("PM"), 8.0, -1.0, Op.is_lt, Op.mult)
+    act(row("D16"), ind(A("PAT", 0, 16), CU("PML")))
+    ts(CF("HA"), COL("H"), float(C), None, Op.mult)
+    ts(CF("HB"), COL("H"), -float(C), float(C), Op.mult, Op.add)
+    ts(CF("I4Y"), CF("I4"), 4.0 / PACK, None, Op.mult)
+    ts(CF("I4F"), CF("I4"), 4.0, None, Op.mult)
+    ts(CF("TA"), COL("T4"), 0.125, None, Op.add)
+    ts(CF("TB"), COL("T4"), 4 * HALF + 0.125, None, Op.add)
+    ts(CU("UL", 8), CF("UW", 8), COL("PM"), None, Op.add)
+    ts(CF("CY", 32), CF("CX", 32), COL("P32"), None, Op.add)
+    ts(A("QC", 1, 36, 2), CF("CW", 18), 0.25, None, Op.add)
+
     cp(A("AU0", 0, 18), LI("pb"))
     send(rank ^ MASK[0], A("LP0", 0, 18), A("AU0", 0, 18), "ap0")
-    act(A("A0B", 0, 288), CF("A0", 288))
-    act(A("A0B", 288, 576), CF("A0", 288))
-    cp(CU("ULU", 32), LI("UL", 32))
-    ts(CF("CW"), CF("KW"), CF("PMF", 1), None, Op.add)
-    for i in range(3):
-        ts(A("AB", 18 * i, 18 * i + 18), CF("CW"), 0.25, None, Op.add)
-
-    planar(0, 0, C)
-
-    def onehot(b):
+    for b in range(4):
         emit("G", lambda e: e.affine_select(T.ET[:, 512 * b:512 * b + 512], T.ONE[:, :], [[-1, 512]], Op.is_equal, 0.0, b, 4),
              [A("ET", 512 * b, 512 * b + 512)], [A("ONE", 0, 512)])
-
-    for b in range(4):
-        onehot(b)
-
-    cp(CU("LGU"), LI("lg"))
     cp(CU("FU"), LI("fd"))
-    chain("YR0", 0, CF("IOT", 288), "CU", _U["LGU"], False)
-    def stand(j, n):
-        off, o = CU("ULU", 8 * n, 8 * j), (128 * j, 128 * (j + n))
-        emit("V", lambda e: e.tensor_copy(T.uq2[:, o[0]:o[1]].bitcast(dt.uint32),
-                                          T.uq[:, 0:128].bitcast(dt.uint32).indirect(off[0])),
-             [A("uq2", o[0], o[1])], [A("uq", 0, 128), off])
-        emit("S", lambda e: e.activation(T.us2[:, o[0]:o[1]], T.us[:, 0:128].indirect(off[0]), Act.Copy),
-             [A("us2", o[0], o[1])], [A("us", 0, 128), off])
-
-    cp(CF("EXF"), LI("ex"))
+    ts(A("QO0", 1, 36, 2), LI("pb"), 0.25, None, Op.add)
+    act(row("WA"), ind(CF("IOT", C), CU("FU")))
     quant("uq", "us", 0, 128, A("ut", 0, 512))
-    tt(CF("LOWF"), CF("EXF"), CF("CW"), Op.min)
-    tt(CF("D1"), CF("EXF"), CF("CW"), Op.subtract)
-    stand(1, 2)
-    cp(A("LU", 18, 36), CF("LOWF"))
-    quant("XQ0", "XS0", 0, 288, A("X0", 0, 1152))
-    chain("YG", 0, A("YR0", 0, 288), "CU", _U["FU"], False)
-    stand(0, 1)
-    stand(3, 1)
-    for j in (2, 1, 0, 3):
-        mm(j, "uq2", "us2", 128 * j, "XQ0", "XS0", 0, 288)
-    for i in range(3):
-        ts(A("DP", 18 * i, 18 * i + 18), CF("D1"), CF("INV", 1), None, Op.mult)
+    tt(CF("PK", C), ind(CF("IOT", C), CU("FU")), CF("IOB", C), Op.add)
+    act(row("WB"), ind(row("WA"), CU("FU")))
+    emit("V", lambda e: e.tensor_copy(T.uq2[:, 0:128].bitcast(dt.uint32), T.uq[:, 0:128].bitcast(dt.uint32).indirect(CU("UL", 8)[0])),
+         [A("uq2", 0, 128)], [A("uq", 0, 128), CU("UL", 8)])
+    emit("S", lambda e: e.activation(T.us2[:, 0:128], T.us[:, 0:128].indirect(CU("UL", 8)[0]), Act.Copy),
+         [A("us2", 0, 128)], [A("us", 0, 128), CU("UL", 8)])
+    small("RA", row("WB"), CU("FU"))
+    act(row("WC"), ind(CF("IOT", C), A("AU0", 0, 18)))
+    quant("XQ0", "XS0", 0, C, A("X0", 0, 1152))
+    cp(CU("EXU"), A("EXW", EX, EX + 18))
+    tt(CF("LX", 32), ind(A("EXW", 0, 96), CU("GL", 2)), CF("CY", 32), Op.min)
+    small("RE", row("WC"), CU("EXU"))
+    tt(A("QC", 0, 36, 2), A("EXW", EX, EX + 18), CF("CW", 18), Op.subtract)
+    ts(CU("L", 18, 0, 2), A("CF", _F["LX"], _F["LX"] + 18, 2), CF("HA"), None, Op.add)
+    ts(CU("L", 18, 1, 2), A("CF", _F["LX"] + 1, _F["LX"] + 18, 2), CF("HB"), None, Op.add)
 
-    def msig(q, j, lo, hi):
-        o, i = A("M", 288 * j + lo, 288 * j + hi), BANK(j, hi - lo)
+    def scores(xq, xs, lo, hi, q):
+        mm(0, "uq", "us", 0, xq, xs, lo, hi)
+        mm(1, "uq2", "us2", 0, xq, xs, lo, hi)
         if q == "V":
-            ts(o, i, 0.0, None, Op.is_lt)
+            ts(A("M", lo, hi), BANK(0, hi - lo), 0.0, CF("MSK"), Op.is_lt, Op.mult)
         else:
-            act(o, i, Act.Sign, -1.0)
+            act(A("M", lo, hi), BANK(0, hi - lo), Act.Sign, CF("NMS"))
+        act(A("M", C + lo, C + hi), BANK(1, hi - lo), Act.Sign, CF("NMS"))
 
-    def rbit(q, j, lst):
-        s = SLOT[j]
-        o, i = A("RB", 288 * s, 288 * s + 288), ind(A("M", 288 * j, 288 * j + 288), lst)
-        if q == "V":
-            ts(o, i, 0.0, None, Op.max)
-        else:
-            act(o, i, Act.Relu)
+    def choose(j, out, pair):
+        scan(out, A("TR", 24 + j, 305 + j, 8), pair)
 
-    def choose(s, n, at, between=()):
-        a, b = A("QS", 18 * s, 18 * (s + n)), A("QS", 72 + 18 * s, 72 + 18 * (s + n))
-        steps = [lambda: scan(A("SB", 288 * s, 288 * (s + n)), A("RB", 288 * s, 288 * (s + n)), 288 * n, bits=True),
-                 lambda: tt(a, E16("SB", 288 * s, 288 * (s + n)), A("DP", at, at + 18 * n), Op.mult),
-                 lambda: tt(b, a, A("AB", at, at + 18 * n), Op.add),
-                 lambda: cp(A("TU", 18 * s, 18 * (s + n)), b)]
-        for i, step in enumerate(steps):
-            step()
-            if i < len(between):
-                between[i]()
+    def listed(out, a):
+        cp(out, A(a[1][0][0], a[1][0][1] + 1, a[1][0][2], 2))
 
-    LOW = A("LU", 18, 36)
+    def differ(pair):
+        value(CF("TMP", 18), "SE")
+        tt(A(pair, 0, 36, 2), CF("TMP", 18), A(pair, 1, 36, 2), Op.subtract)
+
+    scores("XQ0", "XS0", 0, C, "V")
+    wrap("SE", "RE")
+    wrap("SA", "RA")
+    differ("QO0")
+    value(CU("F3U"), "SA")
+    cp(CU("LGU"), LI("lg"))
 
     for r in range(3):
         other = rank ^ MASK[r]
-        x, xn, last = "X%d" % r, "X%d" % (r + 1), r == 2
-        v, vc, z, h, hp = "V%d" % r, "VC%d" % r, "Z%d" % r, "H%d" % r, "HP%d" % r
-        ks, kl, ko, au, lp = "KS%d" % r, "KL%d" % r, "KO%d" % r, "AU%d" % r, "LP%d" % r
-        yn = "PLB" if last else "YR%d" % (r + 1)
-        yrow = A(yn, 0, 288)
-        pp = A("PP", 0, 288)
+        nr, last = r + 1, r == 2
+        x, xn, z, h, hp = "X%d" % r, "X%d" % nr, "Z%d" % r, "H%d" % r, "HP%d" % r
+        ks, kl, lp = "KS%d" % r, "KL%d" % r, "LP%d" % r
+        own, new = A("QO%d" % r, 0, 36), A("QO%d" % nr, 0, 36)
+        q2, q1, q0 = A("QS", 0, 36), A("QS", 36, 72), A("QS", 72, 108)
+        t2, t1, t0 = A("TU", 0, 18), A("TU", 18, 36), A("TU", 36, 54)
+        ts(A("RB", 0, 160), ind(A("M", 0, 576), CU("L", 10)), 0.0, None, Op.max)
+        act(A("RB", 160, C), ind(A("M", 0, 576), CU("L", 18, 10)), Act.Relu)
         if r == 0:
-            msig("V", 2, 0, C)
-            msig("S", 1, 0, C)
-            chain("YF", 0, A("YG", 0, 288), "CU", _U["FU"], "V")
-            rbit("V", 2, LOW)
-            rbit("S", 1, LOW)
-            msig("S", 0, 0, C)
-            rbit("S", 0, LOW)
-            act(CF("FR", 288), ind(CF("IOT", 288), CU("FU")))
-            choose(0, 2, 0, (lambda: chain("ROW0", 288, A("YF", 0, 288), "CU", _U["FU"], "V"),
-                             lambda: scan(A("SR", 288, 576), A("ROW0", 288, 576), 288)))
-            choose(2, 1, 36, (lambda: chain("WA", 0, CF("IOT", 288), "TU", 0),
-                              lambda: value(A("AU0", 18, 36), "SR", 288, 576),
-                              lambda: chain("WB", 0, A("WA", 0, 288), "AU0", 0)))
-            chain("WA", 0, A("WB", 0, 288), "TU", 18)
-            chain("WB", 0, A("WA", 0, 288), lp, 0)
-            chain("WA", 0, A("WB", 0, 288), "TU", 36)
-            chain("YF", 0, A("WA", 0, 288), "AU0", 18)
-            chain("PP", 0, CF("IOT", 288), lp, 0, False)
-            scan(A("SY", 0, 288), A("YF", 0, 288), 288)
-            value(A("YW", 0, 18), "SY", 0, 288)
-            chain(yn, 0, pp, "YW", 0)
+            ts(A("XH", 0, 576), A(x, 0, 576), 0.5, None, Op.mult)
+            act(row("PP"), ind(CF("PK", C), A(lp, 0, 18)))
         else:
-            msig("V", 2, 0, HALF)
-            msig("S", 1, 0, HALF)
-            rbit("V", 2, A("LU", 0, 18))
-            rbit("S", 1, LOW)
-            msig("S", 0, 0, HALF)
-            chain("PP", 0, CF("IOT", 288), lp, 0, False)
-            choose(0, 2, 0)
-            rbit("S", 0, A("LU", 36, 54))
-            chain("WA", 0, pp, "TU", 0)
-            choose(2, 1, 36)
-            chain("WB", 0, A("WA", 0, 288), "TU", 18, False)
-            chain("WA", 0, A("WB", 0, 288), lp, 0)
-            chain(yn, 0, A("WA", 0, 288), "TU", 36)
-        scan(A("SY", 0, 288), yrow, 288)
-        value(A("YW", 0, 18), "SY", 0, 288)
-
-        def gv(t):
-            act(A(v, 288 * t, 288 * t + 288), ind(A("XP%d" % r, 288 * t, 288 * t + 288), A("YW", 0, 18)), Act.Copy, 0.5)
-
-        def gz(t, a, b):
-            f = CU("FU") if (a, b) == (0, C) else CU("FH", 9, 10 * (a // HALF))
-            w = A(v, 288 * t, 288 * t + 288)
-            tt(A(z, 4 * a, 4 * b, t), ind(w, f), A(vc, 288 * t + a, 288 * t + b), Op.add)
-
-        def gc(q, t):
-            move(q, A(vc, 288 * t, 288 * t + 288), A(v, 288 * t, 288 * t + 288))
-
-        act(A("KR", 0, 144), ind(CF("FR", 288), A("YW", 0, 9)))
-        ts(A(v, 0, 288), ind(A("XP%d" % r, 0, 288), A("YW", 0, 18)), 0.5, None, Op.mult)
-        scan(A("KC", 0, 144), A("KR", 0, 144), 144)
-        gc("V", 0)
-        value(A(ks, 0, 9), "KC", 0, 144)
-        for t in (1, 2, 3):
-            gv(t)
-        gc("V", 1)
-        send(other, A(kl, 0, 9), A(ks, 0, 9), "ak%d" % r)
+            act(A("XH", 0, 576), A(x, 0, 576), Act.Copy, 0.5)
+        emit("V", lambda e: e.transpose(T.TR[:, 32:320], T.RB[:, 0:C]), [A("TR", 32, 320)], [row("RB")])
         if r == 0:
-            cp(CU("FH", 9, 0), A("LI", _L["fd"], _L["fd"] + 9))
-            cp(CU("FH", 9, 10), A("LI", _L["fd"] + 9, _L["fd"] + 18))
-        for t in (2, 3):
-            gc("S", t)
-        msig("S", 3, 0, C if r == 0 else HALF)
-        rbit("S", 3, LOW)
-        act(A("KR", 144, 304), ind(CF("FR", 288), A("YW", 8, 18)))
+            ts(A("XH", 576, 1152), A(x, 576, 1152), 0.5, None, Op.mult)
+        choose(2, q2, A("QC", 0, 36))
+        choose(1, q1, own)
+        listed(t2, q2)
+        choose(0, q0, A("QC" if r == 0 else "QP", 0, 36))
+        listed(t1, q1)
+        step("WA", row("PP"), t2)
+        listed(t0, q0)
+        choose(3, new, own)
+        step("WB", row("WA"), t1)
+        listed(A("AU%d" % nr, 0, 18), new)
+        if not last:
+            send(rank ^ MASK[nr], A("LP%d" % nr, 0, 18), A("AU%d" % nr, 0, 18), "ap%d" % nr)
+            ts(CF("SG", 18), A("TR", 35, 320, 16), -2.0, 1.0, Op.mult, Op.add)
+        if r == 0:
+            step("WA", row("WB"), A(lp, 0, 18))
+            tt(A("QO1", 0, 36, 2), A("QO1", 0, 36, 2), CF("SG", 18), Op.mult)
+            step("WB", row("WA"), t0)
+            step("WA", row("WB"), CU("LGU"))
+            step("YR", row("WA"), CU("F3U"))
+        else:
+            step("WA", row("WB"), t0)
+            if not last:
+                tt(A("QO%d" % nr, 0, 36, 2), A("QO%d" % nr, 0, 36, 2), CF("SG", 18), Op.mult)
+            step("YR", row("WA"), A("AL", 0, 18))
+        scan(row("SY"), row("D4"), row("YR"))
+        small("RF", row("YR"), CU("FU"), 1.0 / PACK)
+        ts(A("Y4", 0, 72), A("SY", 3, C, 4), CF("I4Y"), CF("TA"), Op.mult, Op.add)
+        ts(A("KI", 0, 72), A("SY", 3, C, 4), CF("I4"), None, Op.mult)
+        scan(row("SF"), row("D4"), row("RF"))
+        ts(A("KI", 72, 144), A("KI", 0, 72), int(PACK) - 1, None, Op.bitwise_and)
+        ts(A("YF4", 0, 72), A("SF", 3, C, 4), CF("I4F"), CF("TB"), Op.mult, Op.add)
+        ts(A(ks, 0, 72), A("KI", 72, 144), 4.0, CF("TA"), Op.mult, Op.add)
+        send(other, A(kl, 0, 36), A(ks, 0, 36), "ak%d" % r)
         zq, zs = "ZQ%d" % r, "ZS%d" % r
-        for t in (0, 1, 2):
-            gz(t, 0, C)
-        gz(3, 0, HALF)
-        quant(zq, zs, 0, HALF, A(z, 0, 576))
-        gz(3, HALF, C)
-        quant(zq, zs, HALF, C, A(z, 576, 1152))
 
-        def ev(q, hf, b):
-            o, i = A(h, 288 * b + 144 * hf, 288 * b + 144 * hf + 144), BANK(4 * hf + b, HALF)
+        def ev(q, a, b, e):
+            o, i = A(h, 4 * a + e, 4 * b, 4), BANK((4 if a else 0) + e, b - a)
             if q == "V":
                 ts(o, i, 0.03125, None, Op.mult)
             else:
                 act(o, i, Act.Copy, 0.03125)
 
-        for b in range(4):
-            mm(b, "wq", "wp", 128 * b, zq, zs, 0, HALF)
-            ev("S", 0, b)
-        for b in range(4):
-            mm(4 + b, "wq", "wp", 128 * b, zq, zs, HALF, C)
-            ev("S" if b < 2 else "V", 1, b)
-        for q, b, at, to in (("S", 0, 0, 9), ("V", 2, 0, 9), ("S", 1, 0, 9), ("V", 3, 0, 4), ("S", 3, 4, 9)):
-            move(q, A(hp, 64 * at, 64 * to, b), ind(A(h, 288 * b, 288 * b + 288), A(kl, at, to)))
+        def layer(a, b):
+            quant(zq, zs, a, b, A(z, 4 * a, 4 * b))
+            for e in range(4):
+                mm((4 if a else 0) + e, "wq", "wp", 128 * e, zq, zs, a, b)
+
+        for a, b in zip(ZCUT, ZCUT[1:]):
+            act(A("V", 16 * a, 16 * b), ind(A(x, 0, 1152), A("Y4", a, b)), Act.Copy, 0.5)
+        for a, b in zip(ZCUT, ZCUT[1:]):
+            tt(A(z, 16 * a, 16 * b), ind(A("XH", 0, 1152), A("YF4", a, b)), A("V", 16 * a, 16 * b), Op.add)
+            if 4 * b == ZMID:
+                layer(0, ZMID)
+        layer(ZMID, C)
+        for e in range(4):
+            ev("S", 0, ZMID, e)
+        for e in range(4):
+            ev("VS"[e % 2], ZMID, C, e)
+        cp(A(hp, 0, C), ind(A(h, 0, 1152), A(kl, 0, 18)))
+        act(A(hp, C, 576), ind(A(h, 0, 1152), A(kl, 18, 36)))
         hq, hs, hl, hm = "HQ%d" % r, "HS%d" % r, "HL%d" % r, "HM%d" % r
         quant(hq, hs, 0, HALF, A(hp, 0, 576))
         send(other, B8(hl, 0, HALF), B8(hq, 0, HALF), "ac%d" % r)
         send(other, A(hm, 0, HALF), A(hs, 0, HALF), "as%d" % r)
-        def own(b):
-            tt(A(xn, 576, 1152, b), ind(A(h, 288 * b, 288 * b + 288), A(ko, 0, 9)), A(x, 576, 1152, b), Op.add)
-
-        nr = r + 1
         xq, xs = "XQ%d" % nr, "XS%d" % nr
-        rown, aun = ("PLB" if last else "ROW%d" % nr), "AU%d" % nr
-        plo = 288 if last else 0
-        prow_old = A("ROW%d" % r, 0, 288)
-        if r == 0:
-            act(prow_old, ind(CF("IOT", 288), A("AU0", 0, 18)))
-        if not last:
-            chain("YG", 0, yrow, "CU", _U["FU"], False)
-        choose(3, 1, 18, (lambda: scan(A("KC", 144, 288), A("KR", 160, 304), 144),
-                          lambda: value(A(ko, 0, 9), "KC", 144, 288), lambda: own(0)))
-        act(A(rown, plo, plo + 288), ind(prow_old, A("TU", 54, 72)))
-        if last:
-            store("Y", T.pl[:, :], (T.PLB[0:128:16, :], [("PLB", 0, 576, None)]))
-            for b in (1, 2, 3):
-                own(b)
-            quant(xq, xs, HALF, C, A(xn, 576, 1152))
-            quant("vq", "vs", 0, 128, A("vt", 0, 512))
-        else:
-            own(1)
-            if r == 0:
-                cp(CU("EXU"), LI("ex"))
-                ts(A("EA", 18, 36), CF("EXF"), 0.25, None, Op.add)
-            chain("YF", 0, A("YG", 0, 288), "CU", _U["FU"], False)
-            chain(rown, 288, A("YF", 0, 288), "CU", _U["FU"], False)
-            own(2)
-            own(3)
-            scan(A("SR", 0, 288), A(rown, 0, 288), 288)
-            quant(xq, xs, HALF, C, A(xn, 576, 1152))
-            value(A("AB", 0, 18), "SR", 0, 288)
-            scan(A("SR", 288, 576), A(rown, 288, 576), 288)
-            cp(A(aun, 0, 18), A("AB", 0, 18))
-            send(rank ^ MASK[nr], A("LP%d" % nr, 0, 18), A(aun, 0, 18), "ap%d" % nr)
-            planar(nr, HALF, C)
-            if r == 0:
-                act(CF("ER", 288), ind(CF("IOT", 288), CU("EXU")))
-            act(A("ERO", 0, 288), ind(CF("ER", 288), A(aun, 0, 18)))
-            value(A("AB", 36, 54), "SR", 288, 576)
-            cp(A(aun, 18, 36), A("AB", 36, 54))
-            act(A("ERO", 288, 576), ind(CF("ER", 288), A(aun, 18, 36)))
-            for j in (2, 1, 0, 3):
-                mm(j, "uq2", "us2", 128 * j, xq, xs, HALF, C)
-                msig("S", j, HALF, C)
-            if r == 0:
-                quant("EQ", "ES", 0, 512, A("ET", 0, 2048))
-            for i, at in ((0, 0), (1, 36)):
-                scan(A("SE", 288 * i, 288 * i + 288), A("ERO", 288 * i, 288 * i + 288), 288)
-                value(A("EA", at, at + 18), "SE", 288 * i, 288 * i + 288)
-
-        def yout(a, b, bank):
-            mm(bank, "vq", "vs", 0, xq, xs, a, b)
-            act(A("YO", a, b), BANK(bank, b - a))
-
-        def osc(q, k, a, b):
-            store(q, T.osc[4 * k:4 * k + 4, a:b], (T[xs][32 * k:32 * k + 4, a:b], [(xs, a, b, None)]))
+        tt(A(xn, 576, 1152), ind(A(h, 0, 1152), A(ks, 36, 72)), A(x, 576, 1152), Op.add)
 
         def stores(a, b):
-            yout(a, b, a // HALF)
+            bank = 2 + a // HALF
+            mm(bank, "vq", "vs", 0, xq, xs, a, b)
+            act(A("YO", a, b), BANK(bank, b - a))
             store("Y", T.oc[:, 4 * a:4 * b], B8(xq, a, b))
             store("S", T.y[:, a:b], A("YO", a, b))
             for k in range(4):
-                osc("Y" if k < 3 else "S", k, a, b)
+                store("Y" if k < 3 else "S", T.osc[4 * k:4 * k + 4, a:b], (T[xs][32 * k:32 * k + 4, a:b], [(xs, a, b, 1)]))
 
         if last:
+            act(A("PLB", C, 576), ind(CF("IOT", C), A("AU3", 0, 18)))
+            act(row("WA"), row("YR"), None, 1.0 / PACK, 2.0 ** 23)
+            quant("vq", "vs", 0, 128, A("vt", 0, 512))
+            quant(xq, xs, HALF, C, A(xn, 576, 1152))
+            act(row("PLB"), row("WA"), None, 1.0, -2.0 ** 23)
+            store("Y", T.pl[:, :], (T.PLB[0:128:16, :], [("PLB", 0, 576, 1)]))
             stores(HALF, C)
+        else:
+            lpn = A("LP%d" % nr, 0, 18)
+            act(row("PP"), ind(CF("PK", C), lpn))
+            small("RA", row("YR"), CU("F3U"), 1.0 / PACK)
+            small("RE", row("PP"), CU("EXU"), 1.0 / PACK)
+            ts(A("QP", 1, 36, 2), lpn, 0.25, None, Op.add)
+            quant(xq, xs, HALF, C, A(xn, 576, 1152))
+            wrap("SA", "RA")
+            if r == 0:
+                quant("EQ", "ES", 0, 512, A("ET", 0, 2048))
+            wrap("SE", "RE")
+            value(A("AL", 0, 18), "SA")
+            differ("QP")
+            scores(xq, xs, HALF, C, "S")
+            act(A("XH", 576, 1152), A(xn, 576, 1152), Act.Copy, 0.5)
         for b in range(4):
             mm(4 + b, "EQ", "ES", 128 * b, hl, hm, 0, HALF)
-            tt(A(xn, 0, 576, b), A(x, 0, 576, b), BANK(4 + b, HALF), Op.add)
+            tt(A(xn, b, 576, 4), A(x, b, 576, 4), BANK(4 + b, HALF), Op.add)
         quant(xq, xs, 0, HALF, A(xn, 0, 576))
         if last:
             stores(0, HALF)
         else:
-            planar(nr, 0, HALF)
-            tt(A("LF", 0, 54), A("EA", 0, 54), A("AB", 0, 54), Op.min)
-            tt(A("DM", 0, 54), A("EA", 0, 54), A("AB", 0, 54), Op.subtract)
-            cp(A("LU", 0, 54), A("LF", 0, 54))
-            ts(A("DP", 0, 54), A("DM", 0, 54), CF("INV", 1), None, Op.mult)
-            for j in (2, 1, 0, 3):
-                mm(j, "uq2", "us2", 128 * j, xq, xs, 0, HALF)
+            scores(xq, xs, 0, HALF, "V")
     for s in ("cV", "cS", "cT", "cG", "out", "rl"):
         g.wait_ge(T.sem[s], count[s])

@@ -3,24 +3,23 @@ from concourse.mybir import dt, AluOpType as Op, ActivationFunctionType as Act, 
 C, HALF = 288, 144
 MASK = [4, 1, 2]
 K16, K4, PACK = 2.0 ** 30, 2.0 ** 28, 16384.0
-ZCUT = (0, 20, 40, 56, 72)
+ZCUT = (0, 20, 40, 72)
 ZMID = 160
 _F = {}
 _n = 0
-for _name, _w in (("IOT", 288), ("IOB", 288), ("PK", 288), ("KW", 24), ("CW", 24), ("CX", 32), ("CY", 32), ("LX", 32),
-                  ("UW", 8), ("TM4", 16), ("S1", 16), ("S2", 16), ("S3", 8), ("COL", 8), ("TMP", 24), ("SG", 24),
-                  ("PM1", 1), ("MSK", 1), ("NMS", 1), ("HA", 1), ("HB", 1), ("GO", 1), ("I16", 1), ("I4", 1),
+for _name, _w in (("IOT", 288), ("IOB", 288), ("PK", 288), ("KW", 24), ("CW", 24),
+                  ("UW", 8), ("S1", 16), ("S2", 16), ("S3", 8), ("COL", 8), ("TMP", 24), ("SG", 24),
+                  ("PM1", 1), ("MSK", 1), ("NMS", 1), ("HA", 1), ("HB", 1), ("I16", 1), ("I4", 1),
                   ("I4Y", 1), ("I4F", 1), ("TA", 1), ("TB", 1)):
     _F[_name] = _n
     _n += _w
-_COL = {"PM": (0, 15), "P4": (2, 3), "T4": (0, 3), "H": (4, 1), "O": (0, 1), "P32": (0, 31)}
-_L = {"pb": 0, "fd": 24, "lg": 48}
-_U = {"FU": 0, "F3U": 32, "EXU": 64, "LGU": 96, "PML": 128, "UL": 160, "GL": 176, "L": 192}
-UP, EX, DN = 8, 32, 56
+_COL = {"PM": (0, 15), "P4": (2, 3), "T4": (0, 3), "H": (4, 1)}
+_L = {"pb": 0, "fd": 24, "lg": 48, "ex": 72}
+_U = {"FU": 0, "LOW": 32, "EXU": 64, "LGU": 96, "PML": 128, "UL": 160, "L": 192, "L0": 224}
 
 SCRATCH = {
-    "CF": ("sbuf", [128, _n], "float32"), "LI": ("sbuf", [128, 72], "int32"), "CU": ("sbuf", [128, 224], "uint16"),
-    "PI": ("sbuf", [128, 16], "int32"), "EXW": ("sbuf", [128, 96], "int32"), "KI": ("sbuf", [128, 144], "int32"),
+    "CF": ("sbuf", [128, _n], "float32"), "LI": ("sbuf", [128, 96], "int32"), "CU": ("sbuf", [128, 256], "uint16"),
+    "PI": ("sbuf", [128, 16], "int32"), "TM4": ("sbuf", [128, 288], "bfloat16"), "KI": ("sbuf", [128, 144], "int32"),
     "ut": ("sbuf", [128, 512], "bfloat16"), "vt": ("sbuf", [128, 512], "bfloat16"),
     "uq": ("sbuf", [128, 128], "float8_e4m3fn_x4"), "us": ("sbuf", [128, 128], "uint8"),
     "uq2": ("sbuf", [128, 128], "float8_e4m3fn_x4"), "us2": ("sbuf", [128, 128], "uint8"),
@@ -28,11 +27,13 @@ SCRATCH = {
     "wq": ("sbuf", [128, 512], "float8_e4m3fn_x4"), "wp": ("sbuf", [128, 512], "uint8"),
     "ONE": ("sbuf", [128, 512], "bfloat16"), "ET": ("sbuf", [128, 2048], "bfloat16"),
     "EQ": ("sbuf", [128, 512], "float8_e4m3fn_x4"), "ES": ("sbuf", [128, 512], "uint8"),
-    "PAT": ("sbuf", [128, 32], "bfloat16"), "D16": ("sbuf", [128, 288], "bfloat16"), "D4": ("sbuf", [128, 288], "bfloat16"),
+    "PAT": ("sbuf", [128, 16], "bfloat16"), "D16": ("sbuf", [128, 288], "bfloat16"), "D4": ("sbuf", [128, 288], "bfloat16"),
     "M": ("sbuf", [128, 576], "bfloat16"), "RB": ("sbuf", [128, 288], "bfloat16"), "TR": ("sbuf", [128, 320], "bfloat16"),
+    "RL": ("sbuf", [128, 288], "bfloat16"), "RC": ("sbuf", [128, 288], "bfloat16"), "TS": ("sbuf", [128, 320], "bfloat16"),
+    "RP": ("sbuf", [128, 288], "bfloat16"), "RQ": ("sbuf", [128, 288], "bfloat16"), "RM": ("sbuf", [128, 288], "bfloat16"),
     "RA": ("sbuf", [128, 288], "bfloat16"), "RE": ("sbuf", [128, 288], "bfloat16"), "RF": ("sbuf", [128, 288], "bfloat16"),
     "SA": ("sbuf", [128, 288], "bfloat16"), "SE": ("sbuf", [128, 288], "bfloat16"), "SF": ("sbuf", [128, 288], "bfloat16"),
-    "SY": ("sbuf", [128, 288], "float32"), "PP": ("sbuf", [128, 288], "float32"),
+    "SY": ("sbuf", [128, 288], "float32"), "SK": ("sbuf", [128, 288], "float32"), "PP": ("sbuf", [128, 288], "float32"),
     "WA": ("sbuf", [128, 288], "float32"), "WB": ("sbuf", [128, 288], "float32"), "WC": ("sbuf", [128, 288], "float32"),
     "YR": ("sbuf", [128, 288], "float32"), "QC": ("sbuf", [128, 36], "float32"), "QP": ("sbuf", [128, 36], "float32"),
     "QS": ("sbuf", [128, 108], "float32"), "TU": ("sbuf", [128, 54], "uint16"), "AL": ("sbuf", [128, 18], "uint16"),
@@ -54,7 +55,7 @@ for _r in range(3):
                           ("KS", 72, "uint16"), ("KL", 36, "uint16"), ("LP", 18, "uint16")):
         SCRATCH["%s%d" % (_name, _r)] = ("sbuf", [128, _w], _d)
 
-SEMAPHORES = ["cV", "cS", "cT", "cG", "out", "rl"] + ["ld%d" % i for i in range(12)] + \
+SEMAPHORES = ["cV", "cS", "cT", "cG", "out", "rl"] + ["ld%d" % i for i in range(10)] + \
     ["a%s%d" % (k, r) for k in ("k", "p", "c", "s") for r in range(3)]
 
 
@@ -203,8 +204,8 @@ def rank_program(g, core, T, topo):
 
     def step(out, win, off):
         name, lo = off[1][0][0], off[1][0][1]
-        cp(A(out, 0, 160), ind(win, A(name, lo, lo + 10)))
-        act(A(out, 160, C), ind(win, A(name, lo + 10, lo + 18)))
+        act(A(out, 0, 160), ind(win, A(name, lo, lo + 10)))
+        cp(A(out, 160, C), ind(win, A(name, lo + 10, lo + 18)))
 
     def small(out, win, off, scale=1.0):
         act(row(out), ind(win, off), None, scale, -float(HALF))
@@ -215,108 +216,117 @@ def rank_program(g, core, T, topo):
     def value(out, a):
         ts(out, A(a, 15, C, 16), CF("I16"), HALF + 0.25, Op.mult, Op.add)
 
-    fill(A("EXW", 0, 96), 0)
+    def scores(xq, xs, lo, hi, q):
+        bank = 2 if lo else 0
+        mm(bank + 1, "uq2", "us2", 0, xq, xs, lo, hi)
+        mm(bank, "uq", "us", 0, xq, xs, lo, hi)
+        act(A("M", C + lo, C + hi), BANK(bank + 1, hi - lo), Act.Sign, CF("NMS"))
+        if q == "V":
+            ts(A("M", lo, hi), BANK(bank, hi - lo), 0.0, CF("MSK"), Op.is_lt, Op.mult)
+        else:
+            act(A("M", lo, hi), BANK(bank, hi - lo), Act.Sign, CF("NMS"))
+
+    def turn(out, a):
+        emit("V", lambda e: e.transpose(out[0], a[0]), [out], [a])
+
+    def mixed(name):
+        ts(CU(name, 18, 0, 2), A("SF", 0, C, 32), CF("HA"), None, Op.add)
+        ts(CU(name, 18, 1, 2), A("SF", 16, C, 32), CF("HB"), None, Op.add)
+
+    def choose(j, out, pair, bits="TR"):
+        scan(out, A(bits, 24 + j, 305 + j, 8), pair)
+
+    def listed(out, a):
+        cp(out, A(a[1][0][0], a[1][0][1] + 1, a[1][0][2], 2))
+
     load("Y", "ld0", LI("pb"), T.pb[:, :])
-    load("S", "ld3", LI("fd"), T.fd[:, :])
+    load("S", "ld5", LI("lg"), T.lg[:, :])
+    load("Y", "ld3", LI("fd"), T.fd[:, :])
+    load("S", "ld2", LI("ex"), T.ex[:, :])
+    load("Y", "ld4", A("X0", 576, 1152), T.x[:, 576:1152])
     load("S", "ld1", A("ut", 0, 512), T.u[:, :])
-    load("Y", "ld4", A("X0", 0, 1152), T.x[:, :])
-    load("S", "ld2", A("EXW", EX, EX + 18), T.ex[:, :])
-    load("Y", "ld9", (T.EXW[0:112, UP:UP + 18], [("EXW", UP, UP + 18, 1)]), T.ex[16:128, :])
-    load("S", "ld10", (T.EXW[16:128, DN:DN + 18], [("EXW", DN, DN + 18, 1)]), T.ex[0:112, :])
-    load("Y", "ld5", LI("lg"), T.lg[:, :])
+    load("Y", "ld9", A("X0", 0, 576), T.x[:, 0:576])
+    deps("Y", A("X0", 576, 1152)[1], [])
     load("Y", "ld6", B8("wq", 0, 512), T.wc[:, :])
     load("Y", "ld7", A("wp", 0, 512), T.ws[:, :])
     load("Y", "ld8", A("vt", 0, 512), T.v[:, :])
 
     emit("G", lambda e: e.iota(T.PI[:, 0:1], [[0, 1]], 0, 1), [A("PI", 0, 1)], [])
     iota(CF("KW", 18), [[16, 18]], 0)
-    iota(CF("TM4", 16), [[0, 4], [1, 4]], 0)
     iota(CF("IOT", C), [[1, C]], 0)
     iota(CF("UW", 8), [[32, 4], [-16, 2]], 16)
-    iota(CF("CX", 32), [[32, 16], [0, 2]], 0)
+    iota(row("TM4"), [[0, C // 4], [1, 4]], 0)
 
-    fill(A("ONE", 0, 512), 1.0)
-    fill(A("TR", 0, 32), 0.0)
     for i, (a, b) in enumerate(_COL.values()):
         ts(A("PI", 8 + i, 9 + i), A("PI", 0, 1), a, b, Op.logical_shift_right, Op.bitwise_and)
-    cp(CF("COL", 6), A("PI", 8, 14))
+    fill(A("TR", 0, 32), 0.0)
+    fill(A("TS", 0, 32), 0.0)
+    cp(CF("COL", 4), A("PI", 8, 12))
+    fill(A("ONE", 0, 512), 1.0)
     ts(CF("PM1"), COL("PM"), 1.0, None, Op.add)
-    ts(CU("PML"), CF("KW", 18), 0.0, COL("PM"), Op.mult, Op.add)
     ts(CF("CW", 18), CF("KW", 18), COL("PM"), None, Op.add)
-    ts(A("PAT", 16, 32), CF("TM4", 16), COL("P4"), K4, Op.is_gt, Op.mult)
-    ts(CF("S3", 4), CF("TM4", 4), COL("P4"), 1.0 / K4, Op.is_le, Op.max)
-    ts(CF("GO"), COL("H"), COL("O"), DN - EX + 1.0, Op.subtract, Op.mult)
+    ts(CU("PML"), CF("KW", 18), 0.0, COL("PM"), Op.mult, Op.add)
     ts(CF("S1", 16), CF("IOT", 16), COL("PM"), None, Op.is_gt)
     ts(CF("S2", 16), CF("IOT", 16), CF("PM1"), K16, Op.is_equal, Op.mult)
-    emit("V", lambda e: e.tensor_reduce(CF("I4")[0], CF("S3", 4)[0], Ax.X, Op.mult), [CF("I4")], [CF("S3", 4)])
-    act(row("D4"), ind(A("PAT", 16, 32), CU("PML")))
-    act(CF("IOB", C), CF("IOT", C), Act.Copy, PACK)
-    ts(CU("GL", 2), CF("CW", 2), CF("GO"), float(EX), Op.add, Op.add)
-    tt(A("PAT", 0, 16), CF("S1", 16), CF("S2", 16), Op.max)
-    ts(CF("I16"), COL("PM"), 15.0, 1.0 / K16, Op.is_equal, Op.max)
-    ts(CF("MSK"), COL("PM"), 8.0, None, Op.is_lt)
+    ts(CU("UL", 8), CF("UW", 8), COL("PM"), None, Op.add)
     ts(CF("NMS"), COL("PM"), 8.0, -1.0, Op.is_lt, Op.mult)
+    ts(CF("HA"), COL("H"), float(C), HALF + 0.25, Op.mult, Op.add)
+    ts(CF("HB"), COL("H"), -float(C), C + HALF + 0.25, Op.mult, Op.add)
+    tt(A("PAT", 0, 16), CF("S1", 16), CF("S2", 16), Op.max)
+    ts(CF("MSK"), COL("PM"), 8.0, None, Op.is_lt)
     act(row("D16"), ind(A("PAT", 0, 16), CU("PML")))
-    ts(CF("HA"), COL("H"), float(C), None, Op.mult)
-    ts(CF("HB"), COL("H"), -float(C), float(C), Op.mult, Op.add)
-    ts(CF("I4Y"), CF("I4"), 4.0 / PACK, None, Op.mult)
-    ts(CF("I4F"), CF("I4"), 4.0, None, Op.mult)
     ts(CF("TA"), COL("T4"), 0.125, None, Op.add)
     ts(CF("TB"), COL("T4"), 4 * HALF + 0.125, None, Op.add)
-    ts(CU("UL", 8), CF("UW", 8), COL("PM"), None, Op.add)
-    ts(CF("CY", 32), CF("CX", 32), COL("P32"), None, Op.add)
     ts(A("QC", 1, 36, 2), CF("CW", 18), 0.25, None, Op.add)
+    ts(CF("I16"), COL("PM"), 15.0, 1.0 / K16, Op.is_equal, Op.max)
 
     cp(A("AU0", 0, 18), LI("pb"))
     send(rank ^ MASK[0], A("LP0", 0, 18), A("AU0", 0, 18), "ap0")
+    iota(CF("IOB", C), [[int(PACK), C]], 0)
     for b in range(4):
         emit("G", lambda e: e.affine_select(T.ET[:, 512 * b:512 * b + 512], T.ONE[:, :], [[-1, 512]], Op.is_equal, 0.0, b, 4),
              [A("ET", 512 * b, 512 * b + 512)], [A("ONE", 0, 512)])
+    cp(CU("LGU"), LI("lg"))
+    tt(CF("TMP", 18), LI("ex"), CF("CW", 18), Op.min)
     cp(CU("FU"), LI("fd"))
+    cp(CU("EXU"), LI("ex"))
+    cp(CU("LOW"), CF("TMP", 18))
+    act(row("WA"), ind(CF("IOT", C), CU("LGU")))
+    small("RL", CF("IOT", C), CU("LOW"))
+    ts(CF("S3", 4), A("TM4", 0, 4), COL("P4"), 1.0 / K4, Op.is_le, Op.max)
     ts(A("QO0", 1, 36, 2), LI("pb"), 0.25, None, Op.add)
-    act(row("WA"), ind(CF("IOT", C), CU("FU")))
+    cp(row("WC"), ind(CF("IOT", C), A("AU0", 0, 18)))
+    emit("V", lambda e: e.tensor_reduce(CF("I4")[0], CF("S3", 4)[0], Ax.X, Op.mult), [CF("I4")], [CF("S3", 4)])
     quant("uq", "us", 0, 128, A("ut", 0, 512))
-    tt(CF("PK", C), ind(CF("IOT", C), CU("FU")), CF("IOB", C), Op.add)
-    act(row("WB"), ind(row("WA"), CU("FU")))
+    tt(A("QC", 0, 36, 2), LI("ex"), CF("CW", 18), Op.subtract)
+    ts(CF("I4Y"), CF("I4"), 4.0 / PACK, None, Op.mult)
+    ts(CF("I4F"), CF("I4"), 4.0, None, Op.mult)
     emit("V", lambda e: e.tensor_copy(T.uq2[:, 0:128].bitcast(dt.uint32), T.uq[:, 0:128].bitcast(dt.uint32).indirect(CU("UL", 8)[0])),
          [A("uq2", 0, 128)], [A("uq", 0, 128), CU("UL", 8)])
     emit("S", lambda e: e.activation(T.us2[:, 0:128], T.us[:, 0:128].indirect(CU("UL", 8)[0]), Act.Copy),
          [A("us2", 0, 128)], [A("us", 0, 128), CU("UL", 8)])
-    small("RA", row("WB"), CU("FU"))
-    act(row("WC"), ind(CF("IOT", C), A("AU0", 0, 18)))
-    quant("XQ0", "XS0", 0, C, A("X0", 0, 1152))
-    cp(CU("EXU"), A("EXW", EX, EX + 18))
-    tt(CF("LX", 32), ind(A("EXW", 0, 96), CU("GL", 2)), CF("CY", 32), Op.min)
-    small("RE", row("WC"), CU("EXU"))
-    tt(A("QC", 0, 36, 2), A("EXW", EX, EX + 18), CF("CW", 18), Op.subtract)
-    ts(CU("L", 18, 0, 2), A("CF", _F["LX"], _F["LX"] + 18, 2), CF("HA"), None, Op.add)
-    ts(CU("L", 18, 1, 2), A("CF", _F["LX"] + 1, _F["LX"] + 18, 2), CF("HB"), None, Op.add)
-
-    def scores(xq, xs, lo, hi, q):
-        mm(0, "uq", "us", 0, xq, xs, lo, hi)
-        mm(1, "uq2", "us2", 0, xq, xs, lo, hi)
-        if q == "V":
-            ts(A("M", lo, hi), BANK(0, hi - lo), 0.0, CF("MSK"), Op.is_lt, Op.mult)
-        else:
-            act(A("M", lo, hi), BANK(0, hi - lo), Act.Sign, CF("NMS"))
-        act(A("M", C + lo, C + hi), BANK(1, hi - lo), Act.Sign, CF("NMS"))
-
-    def choose(j, out, pair):
-        scan(out, A("TR", 24 + j, 305 + j, 8), pair)
-
-    def listed(out, a):
-        cp(out, A(a[1][0][0], a[1][0][1] + 1, a[1][0][2], 2))
-
-    def differ(pair):
-        value(CF("TMP", 18), "SE")
-        tt(A(pair, 0, 36, 2), CF("TMP", 18), A(pair, 1, 36, 2), Op.subtract)
-
-    scores("XQ0", "XS0", 0, C, "V")
+    act(row("WB"), ind(row("WA"), CU("FU")))
+    quant("XQ0", "XS0", HALF, C, A("X0", 576, 1152))
+    turn(row("SF"), row("RL"))
+    act(row("WA"), ind(row("WB"), CU("FU")))
+    scores("XQ0", "XS0", HALF, C, "S")
+    ts(row("RE"), ind(row("WC"), CU("EXU")), -float(HALF), None, Op.add)
+    small("RA", row("WA"), CU("FU"))
+    quant("XQ0", "XS0", 0, HALF, A("X0", 0, 576))
+    mixed("L")
     wrap("SE", "RE")
+    tt(CF("PK", C), ind(CF("IOT", C), CU("FU")), CF("IOB", C), Op.add)
+    value(CF("TMP", 18), "SE")
+    scores("XQ0", "XS0", 0, HALF, "V")
+    tt(A("QO0", 0, 36, 2), CF("TMP", 18), A("QO0", 1, 36, 2), Op.subtract)
     wrap("SA", "RA")
-    differ("QO0")
-    value(CU("F3U"), "SA")
-    cp(CU("LGU"), LI("lg"))
+
+    def onehot(r, b):
+        if r == 0:
+            quant("EQ", "ES", 128 * b, 128 * b + 128, A("ET", 512 * b, 512 * b + 512))
+
+    def halve(i, x="X0"):
+        ts(A("XH", C * i, C * i + C), A(x, C * i, C * i + C), 0.5, None, Op.mult)
 
     for r in range(3):
         other = rank ^ MASK[r]
@@ -326,42 +336,43 @@ def rank_program(g, core, T, topo):
         own, new = A("QO%d" % r, 0, 36), A("QO%d" % nr, 0, 36)
         q2, q1, q0 = A("QS", 0, 36), A("QS", 36, 72), A("QS", 72, 108)
         t2, t1, t0 = A("TU", 0, 18), A("TU", 18, 36), A("TU", 36, 54)
-        ts(A("RB", 0, 160), ind(A("M", 0, 576), CU("L", 10)), 0.0, None, Op.max)
-        act(A("RB", 160, C), ind(A("M", 0, 576), CU("L", 18, 10)), Act.Relu)
+        ts(A("RB", 160, C), ind(A("M", 0, 576), CU("L", 18, 10)), 0.0, None, Op.max)
+        act(A("RB", 0, 160), ind(A("M", 0, 576), CU("L", 10)), Act.Relu)
         if r == 0:
-            ts(A("XH", 0, 576), A(x, 0, 576), 0.5, None, Op.mult)
+            value(A("AL", 0, 18), "SA")
             act(row("PP"), ind(CF("PK", C), A(lp, 0, 18)))
         else:
-            act(A("XH", 0, 576), A(x, 0, 576), Act.Copy, 0.5)
-        emit("V", lambda e: e.transpose(T.TR[:, 32:320], T.RB[:, 0:C]), [A("TR", 32, 320)], [row("RB")])
-        if r == 0:
-            ts(A("XH", 576, 1152), A(x, 576, 1152), 0.5, None, Op.mult)
+            act(row("RC"), ind(A("M", 0, 576), CU("L0")), Act.Relu)
+            halve(0, x)
+        turn(A("TR", 32, 320), row("RB"))
+        halve(min(r, 1), x)
         choose(2, q2, A("QC", 0, 36))
         choose(1, q1, own)
         listed(t2, q2)
-        choose(0, q0, A("QC" if r == 0 else "QP", 0, 36))
-        listed(t1, q1)
-        step("WA", row("PP"), t2)
-        listed(t0, q0)
-        choose(3, new, own)
-        step("WB", row("WA"), t1)
-        listed(A("AU%d" % nr, 0, 18), new)
-        if not last:
-            send(rank ^ MASK[nr], A("LP%d" % nr, 0, 18), A("AU%d" % nr, 0, 18), "ap%d" % nr)
-            ts(CF("SG", 18), A("TR", 35, 320, 16), -2.0, 1.0, Op.mult, Op.add)
         if r == 0:
+            choose(0, q0, A("QC", 0, 36))
+            listed(t1, q1)
+            step("WA", row("PP"), t2)
+            listed(t0, q0)
+            ts(row("D4"), row("TM4"), COL("P4"), K4, Op.is_gt, Op.mult)
+            step("WB", row("WA"), t1)
+            halve(1)
             step("WA", row("WB"), A(lp, 0, 18))
-            tt(A("QO1", 0, 36, 2), A("QO1", 0, 36, 2), CF("SG", 18), Op.mult)
+            halve(2)
             step("WB", row("WA"), t0)
-            step("WA", row("WB"), CU("LGU"))
-            step("YR", row("WA"), CU("F3U"))
+            step("YR", row("WB"), A("AL", 0, 18))
+            halve(3)
         else:
-            step("WA", row("WB"), t0)
-            if not last:
-                tt(A("QO%d" % nr, 0, 36, 2), A("QO%d" % nr, 0, 36, 2), CF("SG", 18), Op.mult)
-            step("YR", row("WA"), A("AL", 0, 18))
+            listed(t1, q1)
+            turn(A("TS", 32, 320), row("RC"))
+            step("WA", row("PP"), t2)
+            choose(0, q0, A("QP", 0, 36), "TS")
+            step("WB", row("WA"), t1)
+            listed(t0, q0)
+            step("YR", row("WB"), t0)
         scan(row("SY"), row("D4"), row("YR"))
         small("RF", row("YR"), CU("FU"), 1.0 / PACK)
+        onehot(r, 0)
         ts(A("Y4", 0, 72), A("SY", 3, C, 4), CF("I4Y"), CF("TA"), Op.mult, Op.add)
         ts(A("KI", 0, 72), A("SY", 3, C, 4), CF("I4"), None, Op.mult)
         scan(row("SF"), row("D4"), row("RF"))
@@ -369,6 +380,7 @@ def rank_program(g, core, T, topo):
         ts(A("YF4", 0, 72), A("SF", 3, C, 4), CF("I4F"), CF("TB"), Op.mult, Op.add)
         ts(A(ks, 0, 72), A("KI", 72, 144), 4.0, CF("TA"), Op.mult, Op.add)
         send(other, A(kl, 0, 36), A(ks, 0, 36), "ak%d" % r)
+        onehot(r, 1)
         zq, zs = "ZQ%d" % r, "ZS%d" % r
 
         def ev(q, a, b, e):
@@ -385,18 +397,29 @@ def rank_program(g, core, T, topo):
 
         for a, b in zip(ZCUT, ZCUT[1:]):
             act(A("V", 16 * a, 16 * b), ind(A(x, 0, 1152), A("Y4", a, b)), Act.Copy, 0.5)
+        if not last:
+            act(row("WA"), ind(row("RF"), CU("FU")))
+            act(row("RA"), ind(row("WA"), CU("FU")))
         for a, b in zip(ZCUT, ZCUT[1:]):
             tt(A(z, 16 * a, 16 * b), ind(A("XH", 0, 1152), A("YF4", a, b)), A("V", 16 * a, 16 * b), Op.add)
             if 4 * b == ZMID:
+                choose(3, new, own)
                 layer(0, ZMID)
+        listed(A("AU%d" % nr, 0, 18), new)
         layer(ZMID, C)
+        if not last:
+            send(rank ^ MASK[nr], A("LP%d" % nr, 0, 18), A("AU%d" % nr, 0, 18), "ap%d" % nr)
+            wrap("SA", "RA")
+            value(A("AL", 0, 18), "SA")
         for e in range(4):
-            ev("S", 0, ZMID, e)
+            ev("SSSV"[e], 0, ZMID, e)
         for e in range(4):
-            ev("VS"[e % 2], ZMID, C, e)
+            ev("SVSV"[e], ZMID, C, e)
+        onehot(r, 2)
         cp(A(hp, 0, C), ind(A(h, 0, 1152), A(kl, 0, 18)))
         act(A(hp, C, 576), ind(A(h, 0, 1152), A(kl, 18, 36)))
         hq, hs, hl, hm = "HQ%d" % r, "HS%d" % r, "HL%d" % r, "HM%d" % r
+        onehot(r, 3)
         quant(hq, hs, 0, HALF, A(hp, 0, 576))
         send(other, B8(hl, 0, HALF), B8(hq, 0, HALF), "ac%d" % r)
         send(other, A(hm, 0, HALF), A(hs, 0, HALF), "as%d" % r)
@@ -406,11 +429,12 @@ def rank_program(g, core, T, topo):
         def stores(a, b):
             bank = 2 + a // HALF
             mm(bank, "vq", "vs", 0, xq, xs, a, b)
-            act(A("YO", a, b), BANK(bank, b - a))
             store("Y", T.oc[:, 4 * a:4 * b], B8(xq, a, b))
-            store("S", T.y[:, a:b], A("YO", a, b))
-            for k in range(4):
-                store("Y" if k < 3 else "S", T.osc[4 * k:4 * k + 4, a:b], (T[xs][32 * k:32 * k + 4, a:b], [(xs, a, b, 1)]))
+            (cp if a == 0 else act)(A("YO", a, b), BANK(bank, b - a))
+            if a == 0:
+                for k in range(4):
+                    store("YS"[k // 2], T.osc[4 * k:4 * k + 4, :], (T[xs][32 * k:32 * k + 4, :], [(xs, 0, C, 1)]))
+            store("S" if a == 0 else "Y", T.y[:, a:b], A("YO", a, b))
 
         if last:
             act(A("PLB", C, 576), ind(CF("IOT", C), A("AU3", 0, 18)))
@@ -422,19 +446,19 @@ def rank_program(g, core, T, topo):
             stores(HALF, C)
         else:
             lpn = A("LP%d" % nr, 0, 18)
+            al = A("AL", 0, 18)
+            act(row("RM"), ind(row("RL"), al))
             act(row("PP"), ind(CF("PK", C), lpn))
-            small("RA", row("YR"), CU("F3U"), 1.0 / PACK)
-            small("RE", row("PP"), CU("EXU"), 1.0 / PACK)
-            ts(A("QP", 1, 36, 2), lpn, 0.25, None, Op.add)
+            small("RP", row("PP"), al, 1.0 / PACK)
+            small("RQ", row("PP"), CU("EXU"), 1.0 / PACK)
+            act(row("RE"), ind(row("RQ"), al))
             quant(xq, xs, HALF, C, A(xn, 576, 1152))
-            wrap("SA", "RA")
-            if r == 0:
-                quant("EQ", "ES", 0, 512, A("ET", 0, 2048))
-            wrap("SE", "RE")
-            value(A("AL", 0, 18), "SA")
-            differ("QP")
+            turn(row("SF"), row("RM"))
+            wrap("SA", "RP")
+            mixed("L0")
+            value(A("QP", 1, 36, 2), "SA")
             scores(xq, xs, HALF, C, "S")
-            act(A("XH", 576, 1152), A(xn, 576, 1152), Act.Copy, 0.5)
+            ts(A("XH", 576, 1152), A(xn, 576, 1152), 0.5, None, Op.mult)
         for b in range(4):
             mm(4 + b, "EQ", "ES", 128 * b, hl, hm, 0, HALF)
             tt(A(xn, b, 576, 4), A(x, b, 576, 4), BANK(4 + b, HALF), Op.add)
@@ -442,6 +466,11 @@ def rank_program(g, core, T, topo):
         if last:
             stores(0, HALF)
         else:
+            wrap("SE", "RE")
+            ts(CF("SG", 18), A("TR", 35, 320, 16), -2.0, 1.0, Op.mult, Op.add)
+            value(CF("TMP", 18), "SE")
+            tt(A("QO%d" % nr, 0, 36, 2), A("QO%d" % nr, 0, 36, 2), CF("SG", 18), Op.mult)
             scores(xq, xs, 0, HALF, "V")
+            tt(A("QP", 0, 36, 2), CF("TMP", 18), A("QP", 1, 36, 2), Op.subtract)
     for s in ("cV", "cS", "cT", "cG", "out", "rl"):
         g.wait_ge(T.sem[s], count[s])

from concourse.mybir import dt, AluOpType as Op, ActivationFunctionType as Act, AxisListType as Ax

C, HALF = 288, 144
MASK = [4, 1, 2]
K16, K4, PACK = 2.0 ** 30, 2.0 ** 28, 16384.0
ZCUT = (0, 20, 40, 72)
ZMID = 160
_F = {}
_n = 0
for _name, _w in (("IOT", 288), ("IOB", 288), ("PK", 288), ("KW", 24), ("CW", 24),
                  ("UW", 8), ("S1", 16), ("S2", 16), ("S3", 8), ("COL", 8), ("TMP", 24), ("SG", 24),
                  ("PM1", 1), ("MSK", 1), ("NMS", 1), ("HA", 1), ("HB", 1), ("I16", 1), ("I4", 1),
                  ("I4Y", 1), ("I4F", 1), ("TA", 1), ("TB", 1)):
    _F[_name] = _n
    _n += _w
_COL = {"PM": (0, 15), "P4": (2, 3), "T4": (0, 3), "H": (4, 1)}
_L = {"pb": 0, "fd": 24, "lg": 48, "ex": 72}
_U = {"FU": 0, "LOW": 32, "EXU": 64, "LGU": 96, "PML": 128, "UL": 160, "L": 192, "L0": 224}

SCRATCH = {
    "CF": ("sbuf", [128, _n], "float32"), "LI": ("sbuf", [128, 96], "int32"), "CU": ("sbuf", [128, 256], "uint16"),
    "PI": ("sbuf", [128, 16], "int32"), "TM4": ("sbuf", [128, 288], "bfloat16"), "KI": ("sbuf", [128, 144], "int32"),
    "ut": ("sbuf", [128, 512], "bfloat16"), "vt": ("sbuf", [128, 512], "bfloat16"),
    "uq": ("sbuf", [128, 128], "float8_e4m3fn_x4"), "us": ("sbuf", [128, 128], "uint8"),
    "uq2": ("sbuf", [128, 128], "float8_e4m3fn_x4"), "us2": ("sbuf", [128, 128], "uint8"),
    "vq": ("sbuf", [128, 128], "float8_e4m3fn_x4"), "vs": ("sbuf", [128, 128], "uint8"),
    "wq": ("sbuf", [128, 512], "float8_e4m3fn_x4"), "wp": ("sbuf", [128, 512], "uint8"),
    "ONE": ("sbuf", [128, 512], "bfloat16"), "ET": ("sbuf", [128, 2048], "bfloat16"),
    "EQ": ("sbuf", [128, 512], "float8_e4m3fn_x4"), "ES": ("sbuf", [128, 512], "uint8"),
    "PAT": ("sbuf", [128, 16], "bfloat16"), "D16": ("sbuf", [128, 288], "bfloat16"), "D4": ("sbuf", [128, 288], "bfloat16"),
    "M": ("sbuf", [128, 576], "bfloat16"), "RB": ("sbuf", [128, 288], "bfloat16"), "TR": ("sbuf", [128, 320], "bfloat16"),
    "RL": ("sbuf", [128, 288], "bfloat16"), "RC": ("sbuf", [128, 288], "bfloat16"), "TS": ("sbuf", [128, 320], "bfloat16"),
    "RP": ("sbuf", [128, 288], "bfloat16"), "RQ": ("sbuf", [128, 288], "bfloat16"), "RM": ("sbuf", [128, 288], "bfloat16"),
    "RA": ("sbuf", [128, 288], "bfloat16"), "RE": ("sbuf", [128, 288], "bfloat16"), "RF": ("sbuf", [128, 288], "bfloat16"),
    "SA": ("sbuf", [128, 288], "bfloat16"), "SE": ("sbuf", [128, 288], "bfloat16"), "SF": ("sbuf", [128, 288], "bfloat16"),
    "SY": ("sbuf", [128, 288], "float32"), "SK": ("sbuf", [128, 288], "float32"), "PP": ("sbuf", [128, 288], "float32"),
    "WA": ("sbuf", [128, 288], "float32"), "WB": ("sbuf", [128, 288], "float32"), "WC": ("sbuf", [128, 288], "float32"),
    "YR": ("sbuf", [128, 288], "float32"), "QC": ("sbuf", [128, 36], "float32"), "QP": ("sbuf", [128, 36], "float32"),
    "QS": ("sbuf", [128, 108], "float32"), "TU": ("sbuf", [128, 54], "uint16"), "AL": ("sbuf", [128, 18], "uint16"),
    "Y4": ("sbuf", [128, 72], "uint16"), "YF4": ("sbuf", [128, 72], "uint16"),
    "XH": ("sbuf", [128, 1152], "bfloat16"), "V": ("sbuf", [128, 1152], "bfloat16"),
    "PLB": ("sbuf", [128, 576], "float32"), "YO": ("sbuf", [128, 288], "float32"),
    "PS": ("psum", [128, 4096], "float32"),
}
for _r in range(4):
    SCRATCH["X%d" % _r] = ("sbuf", [128, 1152], "bfloat16")
    SCRATCH["XQ%d" % _r] = ("sbuf", [128, 288], "float8_e4m3fn_x4")
    SCRATCH["XS%d" % _r] = ("sbuf", [128, 288], "uint8")
    SCRATCH["QO%d" % _r] = ("sbuf", [128, 36], "float32")
    SCRATCH["AU%d" % _r] = ("sbuf", [128, 18], "uint16")
for _r in range(3):
    for _name, _w, _d in (("Z", 1152, "bfloat16"), ("H", 1152, "bfloat16"), ("HP", 576, "bfloat16"),
                          ("ZQ", 288, "float8_e4m3fn_x4"), ("ZS", 288, "uint8"), ("HQ", 144, "float8_e4m3fn_x4"),
                          ("HS", 144, "uint8"), ("HL", 144, "float8_e4m3fn_x4"), ("HM", 144, "uint8"),
                          ("KS", 72, "uint16"), ("KL", 36, "uint16"), ("LP", 18, "uint16")):
        SCRATCH["%s%d" % (_name, _r)] = ("sbuf", [128, _w], _d)

SEMAPHORES = ["cV", "cS", "cT", "cG", "out", "rl"] + ["ld%d" % i for i in range(10)] + \
    ["a%s%d" % (k, r) for k in ("k", "p", "c", "s") for r in range(3)]


def rank_program(g, core, T, topo):
    rank = T.rank_of(core)
    if rank is None:
        return
    eng = {"V": g.vector, "S": g.scalar, "T": g.tensor, "G": g, "Y": g.sync}
    csem = {"V": "cV", "S": "cS", "T": "cT", "G": "cG"}
    count = {"cV": 0, "cS": 0, "cT": 0, "cG": 0, "out": 0, "rl": 0}
    know = {q: {} for q in eng}
    uses = {}
    order = [0]

    def A(name, lo, hi, step=1):
        return (T[name][:, lo:hi] if step == 1 else T[name][:, lo:hi:step]), [(name, lo, hi, step)]

    def CF(name, w=1, lo=0):
        return A("CF", _F[name] + lo, _F[name] + lo + w)

    def COL(name):
        return CF("COL", 1, list(_COL).index(name))

    def LI(name):
        return A("LI", _L[name], _L[name] + 18)

    def CU(name, w=18, lo=0, step=1):
        return A("CU", _U[name] + lo, _U[name] + w, step)

    def B8(name, lo, hi):
        return T[name][:, lo:hi].bitcast(dt.uint8), [(name, lo, hi, 1)]

    def ind(win, off):
        return win[0].indirect(off[0]), win[1] + off[1]

    def BANK(i, n):
        return T["PS"][:, 512 * i:512 * i + n], [("PS", i, i + 1, 1)]

    def deps(q, ins, outs):
        found = {}
        for regs, w in ((ins, False), (outs, True)):
            for (name, lo, hi, st) in regs:
                for (l2, h2, s2, w2, op) in uses.get(name, ()):
                    if hi <= l2 or h2 <= lo or (st == s2 and (lo - l2) % st):
                        continue
                    same = op["q"] == q and op["compute"]
                    if name == "PS":
                        if same:
                            continue
                    elif not (w or w2) or (same and w and not w2):
                        continue
                    found[op["n"]] = op
        for n in sorted(found, reverse=True):
            op = found[n]
            if know[q].get(op["sem"], 0) < op["val"]:
                eng[q].wait_ge(T.sem[op["sem"]], op["val"])
                know[q][op["sem"]] = op["val"]
                for s, v in op["know"].items():
                    if know[q].get(s, 0) < v:
                        know[q][s] = v

    def note(op, ins, outs):
        order[0] += 1
        op["n"] = order[0]
        for regs, w in ((ins, False), (outs, True)):
            for (name, lo, hi, st) in regs:
                uses.setdefault(name, []).append((lo, hi, st, w, op))

    def regs_of(args):
        out = []
        for a in args:
            out += a[1]
        return out

    def emit(q, fn, outs, ins):
        ri, ro = regs_of(ins), regs_of(outs)
        deps(q, ri, ro)
        s = csem[q]
        count[s] += 1
        fn(eng[q]).then_inc(T.sem[s], 1)
        note({"q": q, "compute": True, "sem": s, "val": count[s], "know": dict(know[q])}, ri, ro)

    def load(q, sem, dst, src):
        deps(q, [], dst[1])
        eng[q].dma_start(dst[0], src).then_inc(T.sem[sem], 16)
        note({"q": q, "compute": False, "sem": sem, "val": 16, "know": dict(know[q])}, [], dst[1])

    def store(q, dst, src):
        deps(q, src[1], [])
        eng[q].dma_start(dst, src[0]).then_inc(T.sem.out, 16)
        count["out"] += 16

    def send(to, dst, src, sem):
        c = T.cores[to]
        deps("G", src[1], [])
        rid, pid = topo.addr(c, core)
        n = len(topo.engines(core, c))
        g.remote_dma(dst[0], src[0], T.sem[sem], T.sem.rl, pid, rid, topo.mask(core, c))
        count["rl"] += n
        note({"q": "G", "compute": False, "sem": sem, "val": n, "know": {}}, [], dst[1])

    def sc(a):
        return a[0] if isinstance(a, tuple) else a

    def more(*a):
        return [b for b in a if isinstance(b, tuple)]

    def ts(out, in0, s1, s2, op0, op1=None):
        if op1 is None:
            emit("V", lambda e: e.tensor_scalar(out[0], in0[0], sc(s1), None, op0), [out], [in0] + more(s1))
        else:
            emit("V", lambda e: e.tensor_scalar(out[0], in0[0], sc(s1), sc(s2), op0, op1), [out], [in0] + more(s1, s2))

    def tt(out, a, b, op):
        emit("V", lambda e: e.tensor_tensor(out[0], a[0], b[0], op), [out], [a, b])

    def cp(out, a):
        emit("V", lambda e: e.tensor_copy(out[0], a[0]), [out], [a])

    def fill(out, c):
        emit("V", lambda e: e.memset(out[0], c), [out], [])

    def act(out, a, f=Act.Copy, scale=1.0, bias=None):
        if bias is None:
            emit("S", lambda e: e.activation(out[0], a[0], f, scale=sc(scale)), [out], [a] + more(scale))
        else:
            emit("S", lambda e: e.activation(out[0], a[0], Act.Identity, bias=bias, scale=scale), [out], [a])

    def scan(out, d0, d1):
        emit("V", lambda e: e.tensor_tensor_scan(out[0], d0[0], d1[0], 0.0, Op.mult, Op.add), [out], [d0, d1])

    def quant(qn, sn, lo, hi, src):
        a, b = A(qn, lo, hi), A(sn, lo, hi)
        emit("V", lambda e: e.quantize_mx(a[0], b[0], src[0]), [a, b], [src])

    def mm(bank, wn, sn, wlo, xn, pn, lo, hi):
        o = BANK(bank, hi - lo)
        ins = [A(wn, wlo, wlo + 128), A(sn, wlo, wlo + 128), A(xn, lo, hi), A(pn, lo, hi)]
        emit("T", lambda e: e.matmul_mx(o[0], ins[0][0], ins[1][0], ins[2][0], ins[3][0], True, True), [o], ins)

    def iota(out, pattern, base):
        emit("G", lambda e: e.iota(out[0], pattern, base, 0, allow_small_or_imprecise_dtypes=True), [out], [])

    def row(name):
        return A(name, 0, C)

    def step(out, win, off):
        name, lo = off[1][0][0], off[1][0][1]
        act(A(out, 0, 160), ind(win, A(name, lo, lo + 10)))
        cp(A(out, 160, C), ind(win, A(name, lo + 10, lo + 18)))

    def small(out, win, off, scale=1.0):
        act(row(out), ind(win, off), None, scale, -float(HALF))

    def wrap(out, a):
        scan(row(out), row("D16"), row(a))

    def value(out, a):
        ts(out, A(a, 15, C, 16), CF("I16"), HALF + 0.25, Op.mult, Op.add)

    def scores(xq, xs, lo, hi, q):
        bank = 2 if lo else 0
        mm(bank + 1, "uq2", "us2", 0, xq, xs, lo, hi)
        mm(bank, "uq", "us", 0, xq, xs, lo, hi)
        act(A("M", C + lo, C + hi), BANK(bank + 1, hi - lo), Act.Sign, CF("NMS"))
        if q == "V":
            ts(A("M", lo, hi), BANK(bank, hi - lo), 0.0, CF("MSK"), Op.is_lt, Op.mult)
        else:
            act(A("M", lo, hi), BANK(bank, hi - lo), Act.Sign, CF("NMS"))

    def turn(out, a):
        emit("V", lambda e: e.transpose(out[0], a[0]), [out], [a])

    def mixed(name):
        ts(CU(name, 18, 0, 2), A("SF", 0, C, 32), CF("HA"), None, Op.add)
        ts(CU(name, 18, 1, 2), A("SF", 16, C, 32), CF("HB"), None, Op.add)

    def choose(j, out, pair, bits="TR"):
        scan(out, A(bits, 24 + j, 305 + j, 8), pair)

    def listed(out, a):
        cp(out, A(a[1][0][0], a[1][0][1] + 1, a[1][0][2], 2))

    load("Y", "ld0", LI("pb"), T.pb[:, :])
    load("S", "ld5", LI("lg"), T.lg[:, :])
    load("Y", "ld3", LI("fd"), T.fd[:, :])
    load("S", "ld2", LI("ex"), T.ex[:, :])
    load("Y", "ld4", A("X0", 576, 1152), T.x[:, 576:1152])
    load("S", "ld1", A("ut", 0, 512), T.u[:, :])
    load("Y", "ld9", A("X0", 0, 576), T.x[:, 0:576])
    deps("Y", A("X0", 576, 1152)[1], [])
    load("Y", "ld6", B8("wq", 0, 512), T.wc[:, :])
    load("Y", "ld7", A("wp", 0, 512), T.ws[:, :])
    load("Y", "ld8", A("vt", 0, 512), T.v[:, :])

    emit("G", lambda e: e.iota(T.PI[:, 0:1], [[0, 1]], 0, 1), [A("PI", 0, 1)], [])
    iota(CF("KW", 18), [[16, 18]], 0)
    iota(CF("IOT", C), [[1, C]], 0)
    iota(CF("UW", 8), [[32, 4], [-16, 2]], 16)
    iota(row("TM4"), [[0, C // 4], [1, 4]], 0)

    for i, (a, b) in enumerate(_COL.values()):
        ts(A("PI", 8 + i, 9 + i), A("PI", 0, 1), a, b, Op.logical_shift_right, Op.bitwise_and)
    fill(A("TR", 0, 32), 0.0)
    fill(A("TS", 0, 32), 0.0)
    cp(CF("COL", 4), A("PI", 8, 12))
    fill(A("ONE", 0, 512), 1.0)
    ts(CF("PM1"), COL("PM"), 1.0, None, Op.add)
    ts(CF("CW", 18), CF("KW", 18), COL("PM"), None, Op.add)
    ts(CU("PML"), CF("KW", 18), 0.0, COL("PM"), Op.mult, Op.add)
    ts(CF("S1", 16), CF("IOT", 16), COL("PM"), None, Op.is_gt)
    ts(CF("S2", 16), CF("IOT", 16), CF("PM1"), K16, Op.is_equal, Op.mult)
    ts(CU("UL", 8), CF("UW", 8), COL("PM"), None, Op.add)
    ts(CF("NMS"), COL("PM"), 8.0, -1.0, Op.is_lt, Op.mult)
    ts(CF("HA"), COL("H"), float(C), HALF + 0.25, Op.mult, Op.add)
    ts(CF("HB"), COL("H"), -float(C), C + HALF + 0.25, Op.mult, Op.add)
    tt(A("PAT", 0, 16), CF("S1", 16), CF("S2", 16), Op.max)
    ts(CF("MSK"), COL("PM"), 8.0, None, Op.is_lt)
    act(row("D16"), ind(A("PAT", 0, 16), CU("PML")))
    ts(CF("TA"), COL("T4"), 0.125, None, Op.add)
    ts(CF("TB"), COL("T4"), 4 * HALF + 0.125, None, Op.add)
    ts(A("QC", 1, 36, 2), CF("CW", 18), 0.25, None, Op.add)
    ts(CF("I16"), COL("PM"), 15.0, 1.0 / K16, Op.is_equal, Op.max)

    cp(A("AU0", 0, 18), LI("pb"))
    send(rank ^ MASK[0], A("LP0", 0, 18), A("AU0", 0, 18), "ap0")
    iota(CF("IOB", C), [[int(PACK), C]], 0)
    for b in range(4):
        emit("G", lambda e: e.affine_select(T.ET[:, 512 * b:512 * b + 512], T.ONE[:, :], [[-1, 512]], Op.is_equal, 0.0, b, 4),
             [A("ET", 512 * b, 512 * b + 512)], [A("ONE", 0, 512)])
    cp(CU("LGU"), LI("lg"))
    tt(CF("TMP", 18), LI("ex"), CF("CW", 18), Op.min)
    cp(CU("FU"), LI("fd"))
    cp(CU("EXU"), LI("ex"))
    cp(CU("LOW"), CF("TMP", 18))
    act(row("WA"), ind(CF("IOT", C), CU("LGU")))
    small("RL", CF("IOT", C), CU("LOW"))
    ts(CF("S3", 4), A("TM4", 0, 4), COL("P4"), 1.0 / K4, Op.is_le, Op.max)
    ts(A("QO0", 1, 36, 2), LI("pb"), 0.25, None, Op.add)
    cp(row("WC"), ind(CF("IOT", C), A("AU0", 0, 18)))
    emit("V", lambda e: e.tensor_reduce(CF("I4")[0], CF("S3", 4)[0], Ax.X, Op.mult), [CF("I4")], [CF("S3", 4)])
    quant("uq", "us", 0, 128, A("ut", 0, 512))
    tt(A("QC", 0, 36, 2), LI("ex"), CF("CW", 18), Op.subtract)
    ts(CF("I4Y"), CF("I4"), 4.0 / PACK, None, Op.mult)
    ts(CF("I4F"), CF("I4"), 4.0, None, Op.mult)
    emit("V", lambda e: e.tensor_copy(T.uq2[:, 0:128].bitcast(dt.uint32), T.uq[:, 0:128].bitcast(dt.uint32).indirect(CU("UL", 8)[0])),
         [A("uq2", 0, 128)], [A("uq", 0, 128), CU("UL", 8)])
    emit("S", lambda e: e.activation(T.us2[:, 0:128], T.us[:, 0:128].indirect(CU("UL", 8)[0]), Act.Copy),
         [A("us2", 0, 128)], [A("us", 0, 128), CU("UL", 8)])
    act(row("WB"), ind(row("WA"), CU("FU")))
    quant("XQ0", "XS0", HALF, C, A("X0", 576, 1152))
    turn(row("SF"), row("RL"))
    act(row("WA"), ind(row("WB"), CU("FU")))
    scores("XQ0", "XS0", HALF, C, "S")
    ts(row("RE"), ind(row("WC"), CU("EXU")), -float(HALF), None, Op.add)
    small("RA", row("WA"), CU("FU"))
    quant("XQ0", "XS0", 0, HALF, A("X0", 0, 576))
    mixed("L")
    wrap("SE", "RE")
    tt(CF("PK", C), ind(CF("IOT", C), CU("FU")), CF("IOB", C), Op.add)
    value(CF("TMP", 18), "SE")
    scores("XQ0", "XS0", 0, HALF, "V")
    tt(A("QO0", 0, 36, 2), CF("TMP", 18), A("QO0", 1, 36, 2), Op.subtract)
    wrap("SA", "RA")

    def onehot(r, b):
        if r == 0:
            quant("EQ", "ES", 128 * b, 128 * b + 128, A("ET", 512 * b, 512 * b + 512))

    def halve(i, x="X0"):
        ts(A("XH", C * i, C * i + C), A(x, C * i, C * i + C), 0.5, None, Op.mult)

    for r in range(3):
        other = rank ^ MASK[r]
        nr, last = r + 1, r == 2
        x, xn, z, h, hp = "X%d" % r, "X%d" % nr, "Z%d" % r, "H%d" % r, "HP%d" % r
        ks, kl, lp = "KS%d" % r, "KL%d" % r, "LP%d" % r
        own, new = A("QO%d" % r, 0, 36), A("QO%d" % nr, 0, 36)
        q2, q1, q0 = A("QS", 0, 36), A("QS", 36, 72), A("QS", 72, 108)
        t2, t1, t0 = A("TU", 0, 18), A("TU", 18, 36), A("TU", 36, 54)
        ts(A("RB", 160, C), ind(A("M", 0, 576), CU("L", 18, 10)), 0.0, None, Op.max)
        act(A("RB", 0, 160), ind(A("M", 0, 576), CU("L", 10)), Act.Relu)
        if r == 0:
            value(A("AL", 0, 18), "SA")
            act(row("PP"), ind(CF("PK", C), A(lp, 0, 18)))
        else:
            act(row("RC"), ind(A("M", 0, 576), CU("L0")), Act.Relu)
            halve(0, x)
        turn(A("TR", 32, 320), row("RB"))
        halve(min(r, 1), x)
        choose(2, q2, A("QC", 0, 36))
        choose(1, q1, own)
        listed(t2, q2)
        if r == 0:
            choose(0, q0, A("QC", 0, 36))
            listed(t1, q1)
            step("WA", row("PP"), t2)
            listed(t0, q0)
            ts(row("D4"), row("TM4"), COL("P4"), K4, Op.is_gt, Op.mult)
            step("WB", row("WA"), t1)
            halve(1)
            step("WA", row("WB"), A(lp, 0, 18))
            halve(2)
            step("WB", row("WA"), t0)
            step("YR", row("WB"), A("AL", 0, 18))
            halve(3)
        else:
            listed(t1, q1)
            turn(A("TS", 32, 320), row("RC"))
            step("WA", row("PP"), t2)
            choose(0, q0, A("QP", 0, 36), "TS")
            step("WB", row("WA"), t1)
            listed(t0, q0)
            step("YR", row("WB"), t0)
        scan(row("SY"), row("D4"), row("YR"))
        small("RF", row("YR"), CU("FU"), 1.0 / PACK)
        onehot(r, 0)
        ts(A("Y4", 0, 72), A("SY", 3, C, 4), CF("I4Y"), CF("TA"), Op.mult, Op.add)
        ts(A("KI", 0, 72), A("SY", 3, C, 4), CF("I4"), None, Op.mult)
        scan(row("SF"), row("D4"), row("RF"))
        ts(A("KI", 72, 144), A("KI", 0, 72), int(PACK) - 1, None, Op.bitwise_and)
        ts(A("YF4", 0, 72), A("SF", 3, C, 4), CF("I4F"), CF("TB"), Op.mult, Op.add)
        ts(A(ks, 0, 72), A("KI", 72, 144), 4.0, CF("TA"), Op.mult, Op.add)
        send(other, A(kl, 0, 36), A(ks, 0, 36), "ak%d" % r)
        onehot(r, 1)
        zq, zs = "ZQ%d" % r, "ZS%d" % r

        def ev(q, a, b, e):
            o, i = A(h, 4 * a + e, 4 * b, 4), BANK((4 if a else 0) + e, b - a)
            if q == "V":
                ts(o, i, 0.03125, None, Op.mult)
            else:
                act(o, i, Act.Copy, 0.03125)

        def layer(a, b):
            quant(zq, zs, a, b, A(z, 4 * a, 4 * b))
            for e in range(4):
                mm((4 if a else 0) + e, "wq", "wp", 128 * e, zq, zs, a, b)

        for a, b in zip(ZCUT, ZCUT[1:]):
            act(A("V", 16 * a, 16 * b), ind(A(x, 0, 1152), A("Y4", a, b)), Act.Copy, 0.5)
        if not last:
            act(row("WA"), ind(row("RF"), CU("FU")))
            act(row("RA"), ind(row("WA"), CU("FU")))
        for a, b in zip(ZCUT, ZCUT[1:]):
            tt(A(z, 16 * a, 16 * b), ind(A("XH", 0, 1152), A("YF4", a, b)), A("V", 16 * a, 16 * b), Op.add)
            if 4 * b == ZMID:
                choose(3, new, own)
                layer(0, ZMID)
        listed(A("AU%d" % nr, 0, 18), new)
        layer(ZMID, C)
        if not last:
            send(rank ^ MASK[nr], A("LP%d" % nr, 0, 18), A("AU%d" % nr, 0, 18), "ap%d" % nr)
            wrap("SA", "RA")
            value(A("AL", 0, 18), "SA")
        for e in range(4):
            ev("SSSV"[e], 0, ZMID, e)
        for e in range(4):
            ev("SVSV"[e], ZMID, C, e)
        onehot(r, 2)
        cp(A(hp, 0, C), ind(A(h, 0, 1152), A(kl, 0, 18)))
        act(A(hp, C, 576), ind(A(h, 0, 1152), A(kl, 18, 36)))
        hq, hs, hl, hm = "HQ%d" % r, "HS%d" % r, "HL%d" % r, "HM%d" % r
        onehot(r, 3)
        quant(hq, hs, 0, HALF, A(hp, 0, 576))
        send(other, B8(hl, 0, HALF), B8(hq, 0, HALF), "ac%d" % r)
        send(other, A(hm, 0, HALF), A(hs, 0, HALF), "as%d" % r)
        xq, xs = "XQ%d" % nr, "XS%d" % nr
        tt(A(xn, 576, 1152), ind(A(h, 0, 1152), A(ks, 36, 72)), A(x, 576, 1152), Op.add)

        def stores(a, b):
            bank = 2 + a // HALF
            mm(bank, "vq", "vs", 0, xq, xs, a, b)
            store("Y", T.oc[:, 4 * a:4 * b], B8(xq, a, b))
            (cp if a == 0 else act)(A("YO", a, b), BANK(bank, b - a))
            if a == 0:
                for k in range(4):
                    store("YS"[k // 2], T.osc[4 * k:4 * k + 4, :], (T[xs][32 * k:32 * k + 4, :], [(xs, 0, C, 1)]))
            store("S" if a == 0 else "Y", T.y[:, a:b], A("YO", a, b))

        if last:
            act(A("PLB", C, 576), ind(CF("IOT", C), A("AU3", 0, 18)))
            act(row("WA"), row("YR"), None, 1.0 / PACK, 2.0 ** 23)
            quant("vq", "vs", 0, 128, A("vt", 0, 512))
            quant(xq, xs, HALF, C, A(xn, 576, 1152))
            act(row("PLB"), row("WA"), None, 1.0, -2.0 ** 23)
            store("Y", T.pl[:, :], (T.PLB[0:128:16, :], [("PLB", 0, 576, 1)]))
            stores(HALF, C)
        else:
            lpn = A("LP%d" % nr, 0, 18)
            al = A("AL", 0, 18)
            act(row("RM"), ind(row("RL"), al))
            act(row("PP"), ind(CF("PK", C), lpn))
            small("RP", row("PP"), al, 1.0 / PACK)
            small("RQ", row("PP"), CU("EXU"), 1.0 / PACK)
            act(row("RE"), ind(row("RQ"), al))
            quant(xq, xs, HALF, C, A(xn, 576, 1152))
            turn(row("SF"), row("RM"))
            wrap("SA", "RP")
            mixed("L0")
            value(A("QP", 1, 36, 2), "SA")
            scores(xq, xs, HALF, C, "S")
            ts(A("XH", 576, 1152), A(xn, 576, 1152), 0.5, None, Op.mult)
        for b in range(4):
            mm(4 + b, "EQ", "ES", 128 * b, hl, hm, 0, HALF)
            tt(A(xn, b, 576, 4), A(x, b, 576, 4), BANK(4 + b, HALF), Op.add)
        quant(xq, xs, 0, HALF, A(xn, 0, 576))
        if last:
            stores(0, HALF)
        else:
            wrap("SE", "RE")
            ts(CF("SG", 18), A("TR", 35, 320, 16), -2.0, 1.0, Op.mult, Op.add)
            value(CF("TMP", 18), "SE")
            tt(A("QO%d" % nr, 0, 36, 2), A("QO%d" % nr, 0, 36, 2), CF("SG", 18), Op.mult)
            scores(xq, xs, 0, HALF, "V")
            tt(A("QP", 0, 36, 2), CF("TMP", 18), A("QP", 1, 36, 2), Op.subtract)
    for s in ("cV", "cS", "cT", "cG", "out", "rl"):
        g.wait_ge(T.sem[s], count[s])
